import numpy as np
import ml_dtypes


def mxq(x, axis, fmt="e4m3"):
    dtype, down = {"e4m3": (ml_dtypes.float8_e4m3fn, 7), "e5m2": (ml_dtypes.float8_e5m2, 14)}[fmt]
    v = np.moveaxis(np.asarray(x, np.float32).astype(ml_dtypes.bfloat16).astype(np.float64), axis, -1)
    blocks = v.reshape(v.shape[:-1] + (-1, 32))
    amax = np.abs(blocks).max(-1, keepdims=True)
    byte = np.maximum(np.where(amax > 0, np.frexp(amax)[1] - 1 + 127, 0) - down, 1)
    scale = np.exp2(byte - 127.0)
    codes = (blocks / scale).astype(np.float32).astype(dtype).astype(np.float64)
    return np.moveaxis((codes * scale).reshape(v.shape), -1, axis)


WIDE = False


def mx_kscale(k):
    if not WIDE:
        return np.ones(k)
    levels = np.array([10, -10, 5, -5, 0])
    if k % 512:
        return np.exp2(np.random.permutation(np.resize(levels, k // 32))).repeat(32)
    a = np.empty((k // 512, 16))
    for p in range(k // 512):
        a[p, :8] = np.random.permutation(np.resize(levels, 8))
        for g in range(8):
            far = levels[np.abs(levels - a[p, g]) >= 10]
            a[p, g + 8] = far[np.random.randint(len(far))]
    return np.exp2(a.ravel()).repeat(32)


def f64(x):
    return np.asarray(x).astype(np.float64)


def striped(idx):
    return np.tile(idx.reshape(-1, 16).T, (8, 1)).astype(np.uint16)


def unstriped(offs):
    return offs[:16].T.reshape(-1).astype(np.int64)


E2M1 = np.array([0.0, 0.5, 1.0, 1.5, 2.0, 3.0, 4.0, 6.0, -0.0, -0.5, -1.0, -1.5, -2.0, -3.0, -4.0, -6.0])


def pack_weight(w, fmt):
    k, n = w.shape
    w = f64(np.asarray(w, np.float32).astype(ml_dtypes.bfloat16)).reshape(k // 32, 32, n)
    amax = np.abs(w).max(1)
    if fmt == "e4m3":
        byte = np.frexp(amax)[1] - 1 + 127 - 7
    else:
        mant, ex = np.frexp(amax / 6.0)
        byte = np.where(mant > 0.5, ex, ex - 1) + 127
    byte = np.clip(np.where(amax > 0, byte, 1), 1, 254)
    scaled = (w * np.exp2(127.0 - byte)[:, None, :]).reshape(k, n).astype(np.float32)
    by_word = np.ascontiguousarray(scaled.reshape(k // 512, 128, 4, n).transpose(0, 1, 3, 2))
    if fmt == "e4m3":
        words = by_word.astype(ml_dtypes.float8_e4m3fn).view(np.uint8)
    else:
        c = by_word.astype(ml_dtypes.float4_e2m1fn).view(np.uint8) & 0xF
        words = (c[..., 0::2] | (c[..., 1::2] << 4)).reshape(k // 512, 128, 2 * n)
    return np.ascontiguousarray(words), np.ascontiguousarray(byte.astype(np.uint8).reshape(k // 512, 16, n))


def unpack_weight(words, scales, fmt):
    g, _, n = scales.shape
    words = np.ascontiguousarray(words).reshape(g, 128, n, -1)
    if fmt == "e4m3":
        vals = words.view(ml_dtypes.float8_e4m3fn).astype(np.float64)
    else:
        nib = np.empty((g, 128, n, 4), np.uint8)
        nib[..., 0::2] = words & 0xF
        nib[..., 1::2] = words >> 4
        vals = E2M1[nib]
    vals = vals * np.repeat(np.exp2(scales.astype(np.float64) - 127.0), 8, axis=1)[..., None]
    return vals.transpose(0, 1, 3, 2).reshape(g * 512, n)


def silu(v):
    return v / (1.0 + np.exp(-np.maximum(v, -700.0)))


K, T, E, C, H, N = 512, 1536, 12, 128, 512, 128
TOP = 3
PAD = 64


def by_expert(wq, xq):
    return np.concatenate([wq[e].T @ xq[:, e * C:(e + 1) * C] for e in range(E)], axis=1)


def setup_inputs():
    n = np.random.standard_normal
    s = mx_kscale(K)[:, None]
    u = mx_kscale(H)
    slot_token = np.empty(E * C, np.int64); pos = np.tile(E * C + np.arange(T) % PAD, (TOP, 1)); taken = np.zeros(T, np.int64)
    liked = np.random.randn(T)
    for e in np.random.permutation(E):
        free = np.flatnonzero(taken < TOP); pick = np.random.permutation(free[np.argsort(-(liked[free] + np.random.gumbel(size=free.size)))[:C]]); slot_token[e * C:(e + 1) * C] = pick
        pos[taken[pick], pick] = e * C + np.arange(C); taken[pick] += 1
    g = np.random.uniform(0.2, 0.8, (TOP, T))
    w1 = [pack_weight(m, "e2m1") for m in n((E, K, H)) / np.sqrt(K) / s[None] * u[None, None, :]]
    w2 = [pack_weight(m, "e2m1") for m in n((E, H, N)) / np.sqrt(H) / u[None, :, None]]
    return {
        "xT": (n((K, T)) * s).astype(np.float32),
        "w1_words": np.stack([m[0] for m in w1]),
        "w1_scales": np.stack([m[1] for m in w1]),
        "w2_words": np.stack([m[0] for m in w2]),
        "w2_scales": np.stack([m[1] for m in w2]),
        "gate": np.stack([np.tile(r, (N, 1)) for r in g]).astype(np.float32),
        "offs": striped(slot_token),
        "pos1": striped(pos[0]),
        "pos2": striped(pos[1]),
        "pos3": striped(pos[2]),
    }


def reference(xT, w1_words, w1_scales, w2_words, w2_scales, gate, offs, pos1, pos2, pos3):
    idx = unstriped(offs)
    w1 = np.stack([unpack_weight(w1_words[e], w1_scales[e], "e2m1") for e in range(E)])
    w2 = np.stack([unpack_weight(w2_words[e], w2_scales[e], "e2m1") for e in range(E)])
    xq = mxq(f64(xT)[:, idx], 0, "e4m3")
    h = silu(by_expert(w1, xq))
    y = by_expert(w2, mxq(h, 0, "e4m3"))
    y = np.concatenate([y, np.zeros((N, PAD))], axis=1)
    return sum(f64(gate[r]) * y[:, unstriped(p)] for r, p in enumerate((pos1, pos2, pos3)))

@@ -1,0 +1,210 @@
+from contextlib import ExitStack
+
+import concourse.mybir as mybir
+from concourse.masks import make_identity
+
+K, T, E, C, H, N = 512, 1536, 12, 128, 512, 128
+PAD = 64
+S = E * C
+P = 128
+FLOPS = 2 * S * (K * H + H * N)
+
+F32 = mybir.dt.float32
+BF16 = mybir.dt.bfloat16
+I32 = mybir.dt.int32
+U32 = mybir.dt.uint32
+U16 = mybir.dt.uint16
+U8 = mybir.dt.uint8
+FP8X4 = mybir.dt.float8_e4m3fn_x4
+FP4X4 = mybir.dt.float4_e2m1fn_x4
+SILU = mybir.ActivationFunctionType.Silu
+MULT = mybir.AluOpType.mult
+ADD = mybir.AluOpType.add
+
+X_CHUNKS = [512,512,256,256]
+SCALAR_SHARE = {128:48,256:80,512:160}
+GATHER_CUTS = [192,192,256,384,512]
+GROUPS = [2,2,2,2,2,2]
+VECTOR_COPY_GROUPS = [0,1,2]
+Y_GROUPS = [4,4,2,2]
+VECTOR_Y_GROUPS = [0]
+OUT_CHUNKS = [512,512,256,256]
+PE_SUM_CHUNKS = [0,1,2]
+
+
+def spans(widths):
+    out, a = [], 0
+    for w in widths:
+        out.append((a, a + w))
+        a += w
+    return out
+
+
+def tile_moe_ecr_mlp_silu_kernel(
+    tc, xT, w1_words, w1_scales, w2_words, w2_scales, gate, offs, pos1, pos2, pos3, out
+):
+    nc = tc.nc
+    with ExitStack() as ctx:
+        lists = ctx.enter_context(tc.tile_pool(name="lists", bufs=1))
+        keep = ctx.enter_context(tc.tile_pool(name="keep", bufs=1))
+        ring = ctx.enter_context(tc.tile_pool(name="ring", bufs=3))
+        psum_a = ctx.enter_context(tc.psum_pool(name="psum_a", bufs=2))
+        psum_t = ctx.enter_context(tc.psum_pool(name="psum_t", bufs=3))
+        psum_y = ctx.enter_context(tc.psum_pool(name="psum_y", bufs=3))
+
+        offs_sb = lists.tile([P, S // 16], U16, name="offs_sb")
+        pos_sb = [lists.tile([P, T // 16], U16, name="pos_sb%d" % r) for r in range(3)]
+
+        x_codes = keep.tile([P, T], U32, name="x_codes", align_bytes=64)
+        x_scales = keep.tile([P, T], U8, name="x_scales", align_bytes=64)
+        slot_codes = keep.tile([P, S], U32, name="slot_codes", align_bytes=64)
+        slot_scales = keep.tile([P, S], U8, name="slot_scales", align_bytes=64)
+        w1 = keep.tile([P, E, 2 * H], U8, name="w1", align_bytes=64)
+        w1s = keep.tile([P, E, H], U8, name="w1s", align_bytes=64)
+        w2 = keep.tile([P, E, 2 * N], U8, name="w2", align_bytes=64)
+        w2s = keep.tile([P, E, N], U8, name="w2s", align_bytes=64)
+        y = keep.tile([P, S + PAD], F32, name="y", align_bytes=64)
+        zeros = keep.tile([P, PAD], F32, name="zeros")
+        ident = keep.tile([P, P], F32, name="ident", align_bytes=64)
+
+        nc.vector.memset(zeros[:], 0.0)
+        nc.scalar.activation(y[:, S:], zeros[:], SILU)
+        nc.vector.memset(w1s[:].rearrange("p e c -> p (e c)").bitcast(I32), 0)
+        nc.vector.memset(w2s[:].rearrange("p e c -> p (e c)").bitcast(I32), 0)
+        nc.vector.memset(x_scales[:].bitcast(I32), 0)
+        make_identity(nc, ident[:])
+
+        x_rows = xT.rearrange("(p j) t -> p j t", j=4)
+        x_raw = []
+        for n, (a, b) in enumerate(spans(X_CHUNKS)):
+            raw = keep.tile([P, 4, b - a], F32, name="x_raw%d" % n, align_bytes=64)
+            nc.sync.dma_start(raw[:], x_rows[:, :, a:b])
+            x_raw.append(raw)
+        nc.sync.dma_start(offs_sb[:], offs)
+
+        def load_words(dst, src, e0, e1):
+            nc.sync.dma_start(
+                dst[:, e0:e1, :].bitcast(I32),
+                src.bitcast(I32).rearrange("e s p c -> p (e s) c")[:, e0:e1, :],
+            )
+
+        def load_scales(dst, src, e0, e1):
+            rows = src.bitcast(I32).rearrange("e s (q r) c -> r q (e s) c", r=4)
+            for r in range(4):
+                nc.sync.dma_start(dst[r:P:32, e0:e1, :].bitcast(I32), rows[r][:, e0:e1, :])
+
+        load_words(w1, w1_words, 0, 2)
+        load_scales(w1s, w1_scales, 0, 4)
+        load_words(w1, w1_words, 2, 6)
+        load_scales(w1s, w1_scales, 4, E)
+        load_scales(w2s, w2_scales, 0, E)
+        load_words(w2, w2_words, 0, E)
+        load_words(w1, w1_words, 6, E)
+        for r, pos in enumerate((pos1, pos2, pos3)):
+            nc.sync.dma_start(pos_sb[r][:], pos)
+        gates = []
+        for n, (a, b) in enumerate(spans(OUT_CHUNKS)):
+            g = keep.tile([P, 3, b - a], F32, name="gate%d" % n, align_bytes=64)
+            nc.sync.dma_start(g[:], gate.rearrange("r p t -> p r t")[:, :, a:b])
+            gates.append(g)
+
+        for n, (a, b) in enumerate(spans(X_CHUNKS)):
+            w = b - a
+            cut = w - SCALAR_SHARE[w]
+            xb = keep.tile([P, w, 4], BF16, name="xb%d" % n, align_bytes=64)
+            dst = xb[:].rearrange("p (c i) j -> p c j i", i=4)
+            src = x_raw[n][:].rearrange("p j (c i) -> p c j i", i=4)
+            nc.vector.tensor_copy(dst[:, : cut // 4], src[:, : cut // 4])
+            nc.scalar.copy(dst[:, cut // 4 :], src[:, cut // 4 :])
+            nc.vector.quantize_mx(
+                x_codes[:, a:b].bitcast(FP8X4), x_scales[:, a:b], xb[:].rearrange("p t j -> p (t j)")
+            )
+
+        def gather(a, b):
+            idx = offs_sb[:, a // 16 : b // 16]
+            nc.vector.tensor_copy(slot_codes[:, a:b], x_codes[:].indirect(idx))
+            nc.vector.tensor_copy(slot_scales[:, a:b], x_scales[:].indirect(idx))
+
+        h_rows = {}
+        y_banks = {}
+
+        def layer1(e):
+            cols = slice(e * C, (e + 1) * C)
+            acc = psum_a.tile([P, H], F32, name="acc_a")
+            nc.tensor.matmul_mx(
+                acc[:], slot_codes[:, cols].bitcast(FP8X4), slot_scales[:, cols],
+                w1[:, e, :].bitcast(FP4X4), w1s[:, e, :], start=True, stop=True,
+            )
+            h = keep.tile([P, 2, P, 2], BF16, name="h_row%d" % e, align_bytes=64)
+            nc.scalar.activation(h[:], acc[:].rearrange("s (p u d) -> s u p d", u=2, d=2), SILU)
+            h_rows[e] = h
+
+        def layer2(gi, e0, e1):
+            g = e1 - e0
+            turned = psum_t.tile([P, g, 2, C], F32, name="turned")
+            for e in range(e0, e1):
+                words = h_rows[e][:].rearrange("s u p d -> s (u p d)").bitcast(F32)
+                for u in range(2):
+                    nc.tensor.transpose(turned[:, e - e0, u, :], words[:, u * P : (u + 1) * P], ident[:])
+            hb = ring.tile([P, g * C * 4], BF16, name="hb", align_bytes=64)
+            dst = hb[:].bitcast(F32).rearrange("p (e s u) -> p e s u", e=g, u=2)
+            src = turned[:].rearrange("p e u s -> p e s u")
+            if gi in VECTOR_COPY_GROUPS:
+                nc.vector.tensor_copy(dst, src)
+            else:
+                nc.scalar.copy(dst, src)
+            h_codes = ring.tile([P, g * C], U32, name="h_codes", align_bytes=64)
+            h_scales = ring.tile([P, g * C], U8, name="h_scales", align_bytes=64)
+            nc.vector.quantize_mx(h_codes[:].bitcast(FP8X4), h_scales[:], hb[:])
+            for e in range(e0, e1):
+                yi, (y0, y1) = [(i, sp) for i, sp in enumerate(spans(Y_GROUPS)) if sp[0] <= e < sp[1]][0]
+                if e == y0:
+                    y_banks[yi] = psum_y.tile([P, (y1 - y0) * C], F32, name="acc_y")
+                acc = y_banks[yi]
+                cols = slice((e - e0) * C, (e - e0 + 1) * C)
+                nc.tensor.matmul_mx(
+                    acc[:, (e - y0) * C : (e - y0 + 1) * C], w2[:, e, :].bitcast(FP4X4), w2s[:, e, :],
+                    h_codes[:, cols].bitcast(FP8X4), h_scales[:, cols], start=True, stop=True,
+                )
+                if e + 1 == y1:
+                    if yi in VECTOR_Y_GROUPS:
+                        nc.vector.tensor_copy(y[:, y0 * C : y1 * C], acc[:])
+                    else:
+                        nc.scalar.copy(y[:, y0 * C : y1 * C], acc[:])
+
+        done1 = 0
+        for a, b in spans(GATHER_CUTS):
+            gather(a, b)
+            while (done1 + 1) * C <= b:
+                layer1(done1)
+                done1 += 1
+        for gi, (e0, e1) in enumerate(spans(GROUPS)):
+            layer2(gi, e0, e1)
+
+        for n, (a, b) in enumerate(spans(OUT_CHUNKS)):
+            w = b - a
+            prods = []
+            for r in range(3):
+                prod = keep.tile([P, w], F32, name="prod%d_%d" % (n, r), align_bytes=64)
+                nc.vector.tensor_tensor(prod[:], y[:].indirect(pos_sb[r][:, a // 16 : b // 16]), gates[n][:, r, :], MULT)
+                prods.append(prod)
+            res = keep.tile([P, w], F32, name="res%d" % n, align_bytes=64)
+            if n in PE_SUM_CHUNKS:
+                summed = psum_a.tile([P, w], F32, name="acc_a")
+                for blk in range(w // P):
+                    cols = slice(blk * P, (blk + 1) * P)
+                    for r in range(3):
+                        nc.tensor.matmul(summed[:, cols], prods[r][:, cols], ident[:], start=(r == 0), stop=(r == 2), is_transpose=True)
+                flipped = keep.tile([P, w], F32, name="flipped%d" % n, align_bytes=64)
+                nc.scalar.copy(flipped[:], summed[:])
+                back = psum_t.tile([P, w], F32, name="turned")
+                for blk in range(w // P):
+                    cols = slice(blk * P, (blk + 1) * P)
+                    nc.tensor.transpose(back[:, cols], flipped[:, cols], ident[:])
+                nc.scalar.copy(res[:], back[:])
+                nc.scalar.dma_start(out[:, a:b], res[:])
+            else:
+                part = keep.tile([P, w], F32, name="part%d" % n, align_bytes=64)
+                nc.vector.tensor_tensor(part[:], prods[0][:], prods[1][:], ADD)
+                nc.vector.tensor_tensor(res[:], part[:], prods[2][:], ADD)
+                nc.sync.dma_start(out[:, a:b], res[:])

@@ -7,6 +7,7 @@ K, T, E, C, H, N = 512, 1536, 12, 128, 512, 128
 PAD = 64
 S = E * C
 P = 128
+BANK = 512
 FLOPS = 2 * S * (K * H + H * N)
 
 F32 = mybir.dt.float32
@@ -21,15 +22,18 @@ SILU = mybir.ActivationFunctionType.Silu
 MULT = mybir.AluOpType.mult
 ADD = mybir.AluOpType.add
 
-X_CHUNKS = [512,512,256,256]
-SCALAR_SHARE = {128:48,256:80,512:160}
-GATHER_CUTS = [192,192,256,384,512]
-GROUPS = [2,2,2,2,2,2]
-VECTOR_COPY_GROUPS = [0,1,2]
-Y_GROUPS = [4,4,2,2]
-VECTOR_Y_GROUPS = [0]
-OUT_CHUNKS = [512,512,256,256]
-PE_SUM_CHUNKS = [0,1,2]
+X_CHUNKS = [512,512,256,128,128]
+SCALAR_SHARE = {128:64,256:128,512:256}
+GATHER_CUTS = [256,256,256,256,256,256]
+VECTOR_COPY_PAIRS = [0,1,2,6]
+QUANT_GROUPS = [4,2,2,2,1,1]
+Y_GROUPS = [4,4,3,1]
+VECTOR_Y_GROUPS = [1,3]
+A_BANKS = [0,1,2,3,4,5,6,7,0,2,4,6]
+Y_BANKS = [7,2,1,3]
+TURN_GROUPS = [2,2,2,2,2,1,1]
+OUT_CHUNKS = [256,256,256,256,320,192]
+PE_SUM_CHUNKS = [0,1,2,3]
 
 
 def spans(widths):
@@ -47,10 +51,10 @@ def tile_moe_ecr_mlp_silu_kernel(
     with ExitStack() as ctx:
         lists = ctx.enter_context(tc.tile_pool(name="lists", bufs=1))
         keep = ctx.enter_context(tc.tile_pool(name="keep", bufs=1))
-        ring = ctx.enter_context(tc.tile_pool(name="ring", bufs=3))
-        psum_a = ctx.enter_context(tc.psum_pool(name="psum_a", bufs=2))
-        psum_t = ctx.enter_context(tc.psum_pool(name="psum_t", bufs=3))
-        psum_y = ctx.enter_context(tc.psum_pool(name="psum_y", bufs=3))
+        psum = ctx.enter_context(tc.psum_pool(name="psum", bufs=1))
+
+        def bank(b):
+            return psum.tile([P, BANK], F32, name="bank%d" % b)
 
         offs_sb = lists.tile([P, S // 16], U16, name="offs_sb")
         pos_sb = [lists.tile([P, T // 16], U16, name="pos_sb%d" % r) for r in range(3)]
@@ -63,7 +67,12 @@ def tile_moe_ecr_mlp_silu_kernel(
         w1s = keep.tile([P, E, H], U8, name="w1s", align_bytes=64)
         w2 = keep.tile([P, E, 2 * N], U8, name="w2", align_bytes=64)
         w2s = keep.tile([P, E, N], U8, name="w2s", align_bytes=64)
+        h_rows = keep.tile([P, E, 2, P, 2], BF16, name="h_rows", align_bytes=64)
+        h_cols = keep.tile([P, S * 4], BF16, name="h_cols", align_bytes=64)
+        h_codes = keep.tile([P, S], U32, name="h_codes", align_bytes=64)
+        h_scales = keep.tile([P, S], U8, name="h_scales", align_bytes=64)
         y = keep.tile([P, S + PAD], F32, name="y", align_bytes=64)
+        gate_sb = keep.tile([P, 3, T], F32, name="gate_sb", align_bytes=64)
         zeros = keep.tile([P, PAD], F32, name="zeros")
         ident = keep.tile([P, P], F32, name="ident", align_bytes=64)
 
@@ -75,12 +84,12 @@ def tile_moe_ecr_mlp_silu_kernel(
         make_identity(nc, ident[:])
 
         x_rows = xT.rearrange("(p j) t -> p j t", j=4)
-        x_raw = []
-        for n, (a, b) in enumerate(spans(X_CHUNKS)):
-            raw = keep.tile([P, 4, b - a], F32, name="x_raw%d" % n, align_bytes=64)
-            nc.sync.dma_start(raw[:], x_rows[:, :, a:b])
-            x_raw.append(raw)
-        nc.sync.dma_start(offs_sb[:], offs)
+        x_raw = {}
+
+        def load_x(n):
+            a, b = spans(X_CHUNKS)[n]
+            x_raw[n] = keep.tile([P, 4, b - a], F32, name="x_raw%d" % n, align_bytes=64)
+            nc.sync.dma_start(x_raw[n][:], x_rows[:, :, a:b])
 
         def load_words(dst, src, e0, e1):
             nc.sync.dma_start(
@@ -93,20 +102,23 @@ def tile_moe_ecr_mlp_silu_kernel(
             for r in range(4):
                 nc.sync.dma_start(dst[r:P:32, e0:e1, :].bitcast(I32), rows[r][:, e0:e1, :])
 
-        load_words(w1, w1_words, 0, 2)
-        load_scales(w1s, w1_scales, 0, 4)
-        load_words(w1, w1_words, 2, 6)
-        load_scales(w1s, w1_scales, 4, E)
-        load_scales(w2s, w2_scales, 0, E)
-        load_words(w2, w2_words, 0, E)
-        load_words(w1, w1_words, 6, E)
+        load_x(0)
+        nc.sync.dma_start(offs_sb[:], offs)
         for r, pos in enumerate((pos1, pos2, pos3)):
             nc.sync.dma_start(pos_sb[r][:], pos)
-        gates = []
-        for n, (a, b) in enumerate(spans(OUT_CHUNKS)):
-            g = keep.tile([P, 3, b - a], F32, name="gate%d" % n, align_bytes=64)
-            nc.sync.dma_start(g[:], gate.rearrange("r p t -> p r t")[:, :, a:b])
-            gates.append(g)
+        load_x(1)
+        load_x(2)
+        load_x(3)
+        load_x(4)
+        load_words(w1, w1_words, 0, 2)
+        load_scales(w1s, w1_scales, 0, 12)
+        load_words(w1, w1_words, 2, 6)
+        load_words(w1, w1_words, 6, 12)
+        load_scales(w2s, w2_scales, 0, 12)
+        load_words(w2, w2_words, 0, 12)
+        nc.sync.dma_start(gate_sb[:, :, 0:512], gate.rearrange("r p t -> p r t")[:, :, 0:512])
+        nc.sync.dma_start(gate_sb[:, :, 512:1024], gate.rearrange("r p t -> p r t")[:, :, 512:1024])
+        nc.sync.dma_start(gate_sb[:, :, 1024:1536], gate.rearrange("r p t -> p r t")[:, :, 1024:1536])
 
         for n, (a, b) in enumerate(spans(X_CHUNKS)):
             w = b - a
@@ -114,8 +126,10 @@ def tile_moe_ecr_mlp_silu_kernel(
             xb = keep.tile([P, w, 4], BF16, name="xb%d" % n, align_bytes=64)
             dst = xb[:].rearrange("p (c i) j -> p c j i", i=4)
             src = x_raw[n][:].rearrange("p j (c i) -> p c j i", i=4)
-            nc.vector.tensor_copy(dst[:, : cut // 4], src[:, : cut // 4])
-            nc.scalar.copy(dst[:, cut // 4 :], src[:, cut // 4 :])
+            if cut:
+                nc.vector.tensor_copy(dst[:, : cut // 4], src[:, : cut // 4])
+            if cut < w:
+                nc.scalar.copy(dst[:, cut // 4 :], src[:, cut // 4 :])
             nc.vector.quantize_mx(
                 x_codes[:, a:b].bitcast(FP8X4), x_scales[:, a:b], xb[:].rearrange("p t j -> p (t j)")
             )
@@ -125,83 +139,87 @@ def tile_moe_ecr_mlp_silu_kernel(
             nc.vector.tensor_copy(slot_codes[:, a:b], x_codes[:].indirect(idx))
             nc.vector.tensor_copy(slot_scales[:, a:b], x_scales[:].indirect(idx))
 
-        h_rows = {}
-        y_banks = {}
-
         def layer1(e):
             cols = slice(e * C, (e + 1) * C)
-            acc = psum_a.tile([P, H], F32, name="acc_a")
+            acc = bank(A_BANKS[e])[:]
             nc.tensor.matmul_mx(
-                acc[:], slot_codes[:, cols].bitcast(FP8X4), slot_scales[:, cols],
+                acc, slot_codes[:, cols].bitcast(FP8X4), slot_scales[:, cols],
                 w1[:, e, :].bitcast(FP4X4), w1s[:, e, :], start=True, stop=True,
             )
-            h = keep.tile([P, 2, P, 2], BF16, name="h_row%d" % e, align_bytes=64)
-            nc.scalar.activation(h[:], acc[:].rearrange("s (p u d) -> s u p d", u=2, d=2), SILU)
-            h_rows[e] = h
+            nc.scalar.activation(h_rows[:, e], acc.rearrange("s (p u d) -> s u p d", u=2, d=2), SILU)
 
-        def layer2(gi, e0, e1):
+        def turn(gi, e0, e1):
             g = e1 - e0
-            turned = psum_t.tile([P, g, 2, C], F32, name="turned")
+            turned = bank(A_BANKS[e1 - 1])[:, : g * 2 * C].rearrange("p (e u s) -> p e u s", e=g, u=2)
             for e in range(e0, e1):
-                words = h_rows[e][:].rearrange("s u p d -> s (u p d)").bitcast(F32)
+                words = h_rows[:, e].rearrange("s u p d -> s (u p d)").bitcast(F32)
                 for u in range(2):
                     nc.tensor.transpose(turned[:, e - e0, u, :], words[:, u * P : (u + 1) * P], ident[:])
-            hb = ring.tile([P, g * C * 4], BF16, name="hb", align_bytes=64)
-            dst = hb[:].bitcast(F32).rearrange("p (e s u) -> p e s u", e=g, u=2)
-            src = turned[:].rearrange("p e u s -> p e s u")
-            if gi in VECTOR_COPY_GROUPS:
+            dst = h_cols[:, e0 * 4 * C : e1 * 4 * C].bitcast(F32).rearrange("p (e s u) -> p e s u", e=g, u=2)
+            src = turned.rearrange("p e u s -> p e s u")
+            if gi in VECTOR_COPY_PAIRS:
                 nc.vector.tensor_copy(dst, src)
             else:
                 nc.scalar.copy(dst, src)
-            h_codes = ring.tile([P, g * C], U32, name="h_codes", align_bytes=64)
-            h_scales = ring.tile([P, g * C], U8, name="h_scales", align_bytes=64)
-            nc.vector.quantize_mx(h_codes[:].bitcast(FP8X4), h_scales[:], hb[:])
+
+        y_banks = {}
+
+        def quantise(e0, e1):
+            cols = slice(e0 * C, e1 * C)
+            nc.vector.quantize_mx(h_codes[:, cols].bitcast(FP8X4), h_scales[:, cols], h_cols[:, e0 * 4 * C : e1 * 4 * C])
+
+        def layer2(e0, e1):
             for e in range(e0, e1):
                 yi, (y0, y1) = [(i, sp) for i, sp in enumerate(spans(Y_GROUPS)) if sp[0] <= e < sp[1]][0]
                 if e == y0:
-                    y_banks[yi] = psum_y.tile([P, (y1 - y0) * C], F32, name="acc_y")
-                acc = y_banks[yi]
-                cols = slice((e - e0) * C, (e - e0 + 1) * C)
+                    y_banks[yi] = bank(Y_BANKS[yi])
+                acc = y_banks[yi][:, : (y1 - y0) * C]
+                cols = slice(e * C, (e + 1) * C)
                 nc.tensor.matmul_mx(
                     acc[:, (e - y0) * C : (e - y0 + 1) * C], w2[:, e, :].bitcast(FP4X4), w2s[:, e, :],
                     h_codes[:, cols].bitcast(FP8X4), h_scales[:, cols], start=True, stop=True,
                 )
                 if e + 1 == y1:
                     if yi in VECTOR_Y_GROUPS:
-                        nc.vector.tensor_copy(y[:, y0 * C : y1 * C], acc[:])
+                        nc.vector.tensor_copy(y[:, y0 * C : y1 * C], acc)
                     else:
-                        nc.scalar.copy(y[:, y0 * C : y1 * C], acc[:])
+                        nc.scalar.copy(y[:, y0 * C : y1 * C], acc)
 
-        done1 = 0
+        done = 0
         for a, b in spans(GATHER_CUTS):
             gather(a, b)
-            while (done1 + 1) * C <= b:
-                layer1(done1)
-                done1 += 1
-        for gi, (e0, e1) in enumerate(spans(GROUPS)):
-            layer2(gi, e0, e1)
+            while (done + 1) * C <= b:
+                layer1(done)
+                done += 1
+        for gi, (t0, t1) in enumerate(spans(TURN_GROUPS)):
+            turn(gi, t0, t1)
+            for e0, e1 in spans(QUANT_GROUPS):
+                if t0 < e1 <= t1:
+                    quantise(e0, e1)
+        for e0, e1 in spans(QUANT_GROUPS):
+            layer2(e0, e1)
 
         for n, (a, b) in enumerate(spans(OUT_CHUNKS)):
             w = b - a
             prods = []
             for r in range(3):
                 prod = keep.tile([P, w], F32, name="prod%d_%d" % (n, r), align_bytes=64)
-                nc.vector.tensor_tensor(prod[:], y[:].indirect(pos_sb[r][:, a // 16 : b // 16]), gates[n][:, r, :], MULT)
+                nc.vector.tensor_tensor(prod[:], y[:].indirect(pos_sb[r][:, a // 16 : b // 16]), gate_sb[:, r, a:b], MULT)
                 prods.append(prod)
             res = keep.tile([P, w], F32, name="res%d" % n, align_bytes=64)
             if n in PE_SUM_CHUNKS:
-                summed = psum_a.tile([P, w], F32, name="acc_a")
+                summed = bank(n % 2)[:, :w]
                 for blk in range(w // P):
                     cols = slice(blk * P, (blk + 1) * P)
                     for r in range(3):
                         nc.tensor.matmul(summed[:, cols], prods[r][:, cols], ident[:], start=(r == 0), stop=(r == 2), is_transpose=True)
                 flipped = keep.tile([P, w], F32, name="flipped%d" % n, align_bytes=64)
-                nc.scalar.copy(flipped[:], summed[:])
-                back = psum_t.tile([P, w], F32, name="turned")
+                nc.scalar.copy(flipped[:], summed)
+                back = bank(4 + n % 2)[:, :w]
                 for blk in range(w // P):
                     cols = slice(blk * P, (blk + 1) * P)
                     nc.tensor.transpose(back[:, cols], flipped[:, cols], ident[:])
-                nc.scalar.copy(res[:], back[:])
+                nc.scalar.copy(res[:], back)
                 nc.scalar.dma_start(out[:, a:b], res[:])
             else:
                 part = keep.tile([P, w], F32, name="part%d" % n, align_bytes=64)

@@ -22,18 +22,20 @@ SILU = mybir.ActivationFunctionType.Silu
 MULT = mybir.AluOpType.mult
 ADD = mybir.AluOpType.add
 
-X_CHUNKS = [512,512,256,128,128]
-SCALAR_SHARE = {128:64,256:128,512:256}
+X_CHUNKS = [768,384,256,128]
+X_QUANT = [[512,256],[256,128],[256],[128]]
+SCALAR_SHARE = {128:48,256:96,512:192}
 GATHER_CUTS = [256,256,256,256,256,256]
-VECTOR_COPY_PAIRS = [0,1,2,6]
+VECTOR_COPY_PAIRS = [0,1,2,5]
 QUANT_GROUPS = [4,2,2,2,1,1]
-Y_GROUPS = [4,4,3,1]
-VECTOR_Y_GROUPS = [1,3]
-A_BANKS = [0,1,2,3,4,5,6,7,0,2,4,6]
-Y_BANKS = [7,2,1,3]
+Y_GROUPS = [4,4,2,1,1]
+VECTOR_Y_GROUPS = [1,4]
+A_BANKS = [0,1,2,3,4,5,6,7,0,2,5,6]
+TURN_BANKS = [1,3,4,7,2,5,0]
+Y_BANKS = [6,7,1,3,4]
 TURN_GROUPS = [2,2,2,2,2,1,1]
-OUT_CHUNKS = [256,256,256,256,320,192]
-PE_SUM_CHUNKS = [0,1,2,3]
+OUT_CHUNKS = [256,256,256,256,128,256,128]
+PE_SUM_CHUNKS = [0,1,2,3,4]
 
 
 def spans(widths):
@@ -72,13 +74,14 @@ def tile_moe_ecr_mlp_silu_kernel(
         h_codes = keep.tile([P, S], U32, name="h_codes", align_bytes=64)
         h_scales = keep.tile([P, S], U8, name="h_scales", align_bytes=64)
         y = keep.tile([P, S + PAD], F32, name="y", align_bytes=64)
-        gate_sb = keep.tile([P, 3, T], F32, name="gate_sb", align_bytes=64)
+        gate_sb = [keep.tile([P, 3, 512], F32, name="gate_sb%d" % n, align_bytes=64) for n in range(3)]
         zeros = keep.tile([P, PAD], F32, name="zeros")
         ident = keep.tile([P, P], F32, name="ident", align_bytes=64)
 
+        nc.gpsimd.memset(w1s[:, :4].rearrange("p e c -> p (e c)").bitcast(I32), 0)
         nc.vector.memset(zeros[:], 0.0)
         nc.scalar.activation(y[:, S:], zeros[:], SILU)
-        nc.vector.memset(w1s[:].rearrange("p e c -> p (e c)").bitcast(I32), 0)
+        nc.vector.memset(w1s[:, 4:].rearrange("p e c -> p (e c)").bitcast(I32), 0)
         nc.vector.memset(w2s[:].rearrange("p e c -> p (e c)").bitcast(I32), 0)
         nc.vector.memset(x_scales[:].bitcast(I32), 0)
         make_identity(nc, ident[:])
@@ -103,36 +106,39 @@ def tile_moe_ecr_mlp_silu_kernel(
                 nc.sync.dma_start(dst[r:P:32, e0:e1, :].bitcast(I32), rows[r][:, e0:e1, :])
 
         load_x(0)
-        nc.sync.dma_start(offs_sb[:], offs)
-        for r, pos in enumerate((pos1, pos2, pos3)):
-            nc.sync.dma_start(pos_sb[r][:], pos)
         load_x(1)
         load_x(2)
         load_x(3)
-        load_x(4)
+        nc.sync.dma_start(offs_sb[:], offs)
         load_words(w1, w1_words, 0, 2)
-        load_scales(w1s, w1_scales, 0, 12)
-        load_words(w1, w1_words, 2, 6)
-        load_words(w1, w1_words, 6, 12)
+        load_scales(w1s, w1_scales, 0, 4)
+        load_words(w1, w1_words, 2, 4)
+        load_words(w1, w1_words, 4, 6)
+        load_scales(w1s, w1_scales, 4, 12)
+        load_words(w1, w1_words, 6, 8)
+        load_words(w1, w1_words, 8, 12)
         load_scales(w2s, w2_scales, 0, 12)
         load_words(w2, w2_words, 0, 12)
-        nc.sync.dma_start(gate_sb[:, :, 0:512], gate.rearrange("r p t -> p r t")[:, :, 0:512])
-        nc.sync.dma_start(gate_sb[:, :, 512:1024], gate.rearrange("r p t -> p r t")[:, :, 512:1024])
-        nc.sync.dma_start(gate_sb[:, :, 1024:1536], gate.rearrange("r p t -> p r t")[:, :, 1024:1536])
+        for r, pos in enumerate((pos1, pos2, pos3)):
+            nc.sync.dma_start(pos_sb[r][:], pos)
+        nc.sync.dma_start(gate_sb[0][:], gate.rearrange("r p t -> p r t")[:, :, 0:512])
+        nc.sync.dma_start(gate_sb[1][:], gate.rearrange("r p t -> p r t")[:, :, 512:1024])
+        nc.sync.dma_start(gate_sb[2][:], gate.rearrange("r p t -> p r t")[:, :, 1024:1536])
 
         for n, (a, b) in enumerate(spans(X_CHUNKS)):
-            w = b - a
-            cut = w - SCALAR_SHARE[w]
-            xb = keep.tile([P, w, 4], BF16, name="xb%d" % n, align_bytes=64)
-            dst = xb[:].rearrange("p (c i) j -> p c j i", i=4)
-            src = x_raw[n][:].rearrange("p j (c i) -> p c j i", i=4)
-            if cut:
-                nc.vector.tensor_copy(dst[:, : cut // 4], src[:, : cut // 4])
-            if cut < w:
-                nc.scalar.copy(dst[:, cut // 4 :], src[:, cut // 4 :])
-            nc.vector.quantize_mx(
-                x_codes[:, a:b].bitcast(FP8X4), x_scales[:, a:b], xb[:].rearrange("p t j -> p (t j)")
-            )
+            for q0, q1 in spans(X_QUANT[n]):
+                w = q1 - q0
+                cut = w - SCALAR_SHARE[w]
+                xb = keep.tile([P, w, 4], BF16, name="xb%d" % (a + q0), align_bytes=64)
+                dst = xb[:].rearrange("p (c i) j -> p c j i", i=4)
+                src = x_raw[n][:, :, q0:q1].rearrange("p j (c i) -> p c j i", i=4)
+                if cut:
+                    nc.vector.tensor_copy(dst[:, : cut // 4], src[:, : cut // 4])
+                if cut < w:
+                    nc.scalar.copy(dst[:, cut // 4 :], src[:, cut // 4 :])
+                nc.vector.quantize_mx(
+                    x_codes[:, a + q0 : a + q1].bitcast(FP8X4), x_scales[:, a + q0 : a + q1], xb[:].rearrange("p t j -> p (t j)")
+                )
 
         def gather(a, b):
             idx = offs_sb[:, a // 16 : b // 16]
@@ -150,7 +156,7 @@ def tile_moe_ecr_mlp_silu_kernel(
 
         def turn(gi, e0, e1):
             g = e1 - e0
-            turned = bank(A_BANKS[e1 - 1])[:, : g * 2 * C].rearrange("p (e u s) -> p e u s", e=g, u=2)
+            turned = bank(TURN_BANKS[gi])[:, : g * 2 * C].rearrange("p (e u s) -> p e u s", e=g, u=2)
             for e in range(e0, e1):
                 words = h_rows[:, e].rearrange("s u p d -> s (u p d)").bitcast(F32)
                 for u in range(2):
@@ -204,20 +210,19 @@ def tile_moe_ecr_mlp_silu_kernel(
             prods = []
             for r in range(3):
                 prod = keep.tile([P, w], F32, name="prod%d_%d" % (n, r), align_bytes=64)
-                nc.vector.tensor_tensor(prod[:], y[:].indirect(pos_sb[r][:, a // 16 : b // 16]), gate_sb[:, r, a:b], MULT)
+                nc.vector.tensor_tensor(prod[:], y[:].indirect(pos_sb[r][:, a // 16 : b // 16]), gate_sb[a // 512][:, r, a % 512 : a % 512 + w], MULT)
                 prods.append(prod)
             res = keep.tile([P, w], F32, name="res%d" % n, align_bytes=64)
             if n in PE_SUM_CHUNKS:
-                summed = bank(n % 2)[:, :w]
-                for blk in range(w // P):
-                    cols = slice(blk * P, (blk + 1) * P)
-                    for r in range(3):
-                        nc.tensor.matmul(summed[:, cols], prods[r][:, cols], ident[:], start=(r == 0), stop=(r == 2), is_transpose=True)
+                blocks = [slice(k * P, (k + 1) * P) for k in range(w // P)]
+                summed = [bank((a // P + k) % 4)[:, :P] for k in range(w // P)]
+                for r in range(3):
+                    for k, cols in enumerate(blocks):
+                        nc.tensor.matmul(summed[k], prods[r][:, cols], ident[:], start=(r == 0), stop=(r == 2), is_transpose=True)
                 flipped = keep.tile([P, w], F32, name="flipped%d" % n, align_bytes=64)
-                nc.scalar.copy(flipped[:], summed)
                 back = bank(4 + n % 2)[:, :w]
-                for blk in range(w // P):
-                    cols = slice(blk * P, (blk + 1) * P)
+                for k, cols in enumerate(blocks):
+                    nc.scalar.copy(flipped[:, cols], summed[k])
                     nc.tensor.transpose(back[:, cols], flipped[:, cols], ident[:])
                 nc.scalar.copy(res[:], back)
                 nc.scalar.dma_start(out[:, a:b], res[:])

@@ -22,17 +22,17 @@ SILU = mybir.ActivationFunctionType.Silu
 MULT = mybir.AluOpType.mult
 ADD = mybir.AluOpType.add
 
-X_CHUNKS = [768,384,256,128]
-X_QUANT = [[512,256],[256,128],[256],[128]]
-SCALAR_SHARE = {128:48,256:96,512:192}
+X_CHUNKS = [512,512,256,128,128]
+X_QUANT = [[512],[256,256],[256],[128],[128]]
+SCALAR_SHARE = {128:64,256:128,512:256}
 GATHER_CUTS = [256,256,256,256,256,256]
-VECTOR_COPY_PAIRS = [0,1,2,5]
+VECTOR_COPY_PAIRS = [0,1,2,3]
 QUANT_GROUPS = [4,2,2,2,1,1]
 Y_GROUPS = [4,4,2,1,1]
-VECTOR_Y_GROUPS = [1,4]
-A_BANKS = [0,1,2,3,4,5,6,7,0,2,5,6]
-TURN_BANKS = [1,3,4,7,2,5,0]
-Y_BANKS = [6,7,1,3,4]
+VECTOR_Y_GROUPS = [1,3]
+A_BANKS = [0,1,2,3,4,5,6,7,0,2,6,0]
+TURN_BANKS = [1,3,5,7,2,6,4]
+Y_BANKS = [0,2,1,3,5]
 TURN_GROUPS = [2,2,2,2,2,1,1]
 OUT_CHUNKS = [256,256,256,256,128,256,128]
 PE_SUM_CHUNKS = [0,1,2,3,4]
@@ -78,10 +78,9 @@ def tile_moe_ecr_mlp_silu_kernel(
         zeros = keep.tile([P, PAD], F32, name="zeros")
         ident = keep.tile([P, P], F32, name="ident", align_bytes=64)
 
-        nc.gpsimd.memset(w1s[:, :4].rearrange("p e c -> p (e c)").bitcast(I32), 0)
         nc.vector.memset(zeros[:], 0.0)
         nc.scalar.activation(y[:, S:], zeros[:], SILU)
-        nc.vector.memset(w1s[:, 4:].rearrange("p e c -> p (e c)").bitcast(I32), 0)
+        nc.vector.memset(w1s[:].rearrange("p e c -> p (e c)").bitcast(I32), 0)
         nc.vector.memset(w2s[:].rearrange("p e c -> p (e c)").bitcast(I32), 0)
         nc.vector.memset(x_scales[:].bitcast(I32), 0)
         make_identity(nc, ident[:])
@@ -106,21 +105,20 @@ def tile_moe_ecr_mlp_silu_kernel(
                 nc.sync.dma_start(dst[r:P:32, e0:e1, :].bitcast(I32), rows[r][:, e0:e1, :])
 
         load_x(0)
+        nc.sync.dma_start(offs_sb[:], offs)
+        nc.sync.dma_start(pos_sb[0][:], pos1)
         load_x(1)
         load_x(2)
         load_x(3)
-        nc.sync.dma_start(offs_sb[:], offs)
+        load_x(4)
         load_words(w1, w1_words, 0, 2)
-        load_scales(w1s, w1_scales, 0, 4)
-        load_words(w1, w1_words, 2, 4)
-        load_words(w1, w1_words, 4, 6)
-        load_scales(w1s, w1_scales, 4, 12)
-        load_words(w1, w1_words, 6, 8)
-        load_words(w1, w1_words, 8, 12)
+        load_scales(w1s, w1_scales, 0, 12)
+        load_words(w1, w1_words, 2, 6)
+        load_words(w1, w1_words, 6, 12)
         load_scales(w2s, w2_scales, 0, 12)
         load_words(w2, w2_words, 0, 12)
-        for r, pos in enumerate((pos1, pos2, pos3)):
-            nc.sync.dma_start(pos_sb[r][:], pos)
+        nc.sync.dma_start(pos_sb[1][:], pos2)
+        nc.sync.dma_start(pos_sb[2][:], pos3)
         nc.sync.dma_start(gate_sb[0][:], gate.rearrange("r p t -> p r t")[:, :, 0:512])
         nc.sync.dma_start(gate_sb[1][:], gate.rearrange("r p t -> p r t")[:, :, 512:1024])
         nc.sync.dma_start(gate_sb[2][:], gate.rearrange("r p t -> p r t")[:, :, 1024:1536])

@@ -34,8 +34,8 @@ A_BANKS = [0,1,2,3,4,5,6,7,0,2,6,0]
 TURN_BANKS = [1,3,5,7,2,6,4]
 Y_BANKS = [0,2,1,3,5]
 TURN_GROUPS = [2,2,2,2,2,1,1]
-OUT_CHUNKS = [256,256,256,256,128,256,128]
-PE_SUM_CHUNKS = [0,1,2,3,4]
+OUT_CHUNKS = [512,256,256,256,128,128]
+PE_SUM_CHUNKS = [0,1,2,3]
 
 
 def spans(widths):
@@ -213,12 +213,12 @@ def tile_moe_ecr_mlp_silu_kernel(
             res = keep.tile([P, w], F32, name="res%d" % n, align_bytes=64)
             if n in PE_SUM_CHUNKS:
                 blocks = [slice(k * P, (k + 1) * P) for k in range(w // P)]
-                summed = [bank((a // P + k) % 4)[:, :P] for k in range(w // P)]
+                summed = [bank((a // P + k) % 6)[:, :P] for k in range(w // P)]
                 for r in range(3):
                     for k, cols in enumerate(blocks):
                         nc.tensor.matmul(summed[k], prods[r][:, cols], ident[:], start=(r == 0), stop=(r == 2), is_transpose=True)
                 flipped = keep.tile([P, w], F32, name="flipped%d" % n, align_bytes=64)
-                back = bank(4 + n % 2)[:, :w]
+                back = bank(6 + n % 2)[:, :w]
                 for k, cols in enumerate(blocks):
                     nc.scalar.copy(flipped[:, cols], summed[k])
                     nc.tensor.transpose(back[:, cols], flipped[:, cols], ident[:])

@@ -25,17 +25,14 @@ ADD = mybir.AluOpType.add
 X_CHUNKS = [512,512,256,128,128]
 X_QUANT = [[512],[256,256],[256],[128],[128]]
 SCALAR_SHARE = {128:64,256:128,512:256}
-GATHER_CUTS = [256,256,256,256,256,256]
-VECTOR_COPY_PAIRS = [0,1,2,3]
-QUANT_GROUPS = [4,2,2,2,1,1]
-Y_GROUPS = [4,4,2,1,1]
-VECTOR_Y_GROUPS = [1,3]
-A_BANKS = [0,1,2,3,4,5,6,7,0,2,6,0]
-TURN_BANKS = [1,3,5,7,2,6,4]
-Y_BANKS = [0,2,1,3,5]
-TURN_GROUPS = [2,2,2,2,2,1,1]
-OUT_CHUNKS = [512,256,256,256,128,128]
-PE_SUM_CHUNKS = [0,1,2,3]
+PAIRS = E // 2
+CODE_CUTS = [192, 192, 256, 256, 256, 192, 192]
+GROUPS = [2, 2, 2, 2, 2, 1, 1]
+VECTOR_GROUPS = 4
+A_RING = 4
+TURN_LAG = 2
+SUMMED = [[768], [384, 128]]
+SUM_RING = 6
 
 
 def spans(widths):
@@ -69,12 +66,10 @@ def tile_moe_ecr_mlp_silu_kernel(
         w1s = keep.tile([P, E, H], U8, name="w1s", align_bytes=64)
         w2 = keep.tile([P, E, 2 * N], U8, name="w2", align_bytes=64)
         w2s = keep.tile([P, E, N], U8, name="w2s", align_bytes=64)
-        h_rows = keep.tile([P, E, 2, P, 2], BF16, name="h_rows", align_bytes=64)
-        h_cols = keep.tile([P, S * 4], BF16, name="h_cols", align_bytes=64)
-        h_codes = keep.tile([P, S], U32, name="h_codes", align_bytes=64)
+        h_rows = [keep.tile([P, H], BF16, name="h_rows%d" % e, align_bytes=64) for e in range(E)]
         h_scales = keep.tile([P, S], U8, name="h_scales", align_bytes=64)
         y = keep.tile([P, S + PAD], F32, name="y", align_bytes=64)
-        gate_sb = [keep.tile([P, 3, 512], F32, name="gate_sb%d" % n, align_bytes=64) for n in range(3)]
+        gate_sb = [keep.tile([P, 3, T // 2], F32, name="gate_sb%d" % n, align_bytes=64) for n in range(2)]
         zeros = keep.tile([P, PAD], F32, name="zeros")
         ident = keep.tile([P, P], F32, name="ident", align_bytes=64)
 
@@ -119,9 +114,8 @@ def tile_moe_ecr_mlp_silu_kernel(
         load_words(w2, w2_words, 0, 12)
         nc.sync.dma_start(pos_sb[1][:], pos2)
         nc.sync.dma_start(pos_sb[2][:], pos3)
-        nc.sync.dma_start(gate_sb[0][:], gate.rearrange("r p t -> p r t")[:, :, 0:512])
-        nc.sync.dma_start(gate_sb[1][:], gate.rearrange("r p t -> p r t")[:, :, 512:1024])
-        nc.sync.dma_start(gate_sb[2][:], gate.rearrange("r p t -> p r t")[:, :, 1024:1536])
+        for n in range(2):
+            nc.sync.dma_start(gate_sb[n][:], gate.rearrange("r p t -> p r t")[:, :, n * T // 2 : (n + 1) * T // 2])
 
         for n, (a, b) in enumerate(spans(X_CHUNKS)):
             for q0, q1 in spans(X_QUANT[n]):
@@ -138,94 +132,120 @@ def tile_moe_ecr_mlp_silu_kernel(
                     x_codes[:, a + q0 : a + q1].bitcast(FP8X4), x_scales[:, a + q0 : a + q1], xb[:].rearrange("p t j -> p (t j)")
                 )
 
-        def gather(a, b):
-            idx = offs_sb[:, a // 16 : b // 16]
-            nc.vector.tensor_copy(slot_codes[:, a:b], x_codes[:].indirect(idx))
-            nc.vector.tensor_copy(slot_scales[:, a:b], x_scales[:].indirect(idx))
+        def gather(dst, src, a, b):
+            nc.vector.tensor_copy(dst[:, a:b], src[:].indirect(offs_sb[:, a // 16 : b // 16]))
 
         def layer1(e):
             cols = slice(e * C, (e + 1) * C)
-            acc = bank(A_BANKS[e])[:]
+            acc = bank(e % A_RING)[:]
             nc.tensor.matmul_mx(
                 acc, slot_codes[:, cols].bitcast(FP8X4), slot_scales[:, cols],
                 w1[:, e, :].bitcast(FP4X4), w1s[:, e, :], start=True, stop=True,
             )
-            nc.scalar.activation(h_rows[:, e], acc.rearrange("s (p u d) -> s u p d", u=2, d=2), SILU)
+            nc.scalar.activation(h_rows[e][:].rearrange("s (u p d) -> s u p d", u=2, d=2), acc.rearrange("s (p u d) -> s u p d", u=2, d=2), SILU)
 
-        def turn(gi, e0, e1):
-            g = e1 - e0
-            turned = bank(TURN_BANKS[gi])[:, : g * 2 * C].rearrange("p (e u s) -> p e u s", e=g, u=2)
+        groups = spans(GROUPS)
+        turned, h_cols, h_codes = {}, {}, {}
+
+        def turn(g):
+            e0, e1 = groups[g]
+            turned[g] = bank((A_RING + g) % 8)[:, : (e1 - e0) * 2 * C].rearrange("p (e u s) -> p e u s", u=2, s=C)
             for e in range(e0, e1):
-                words = h_rows[:, e].rearrange("s u p d -> s (u p d)").bitcast(F32)
+                words = h_rows[e][:].bitcast(F32)
                 for u in range(2):
-                    nc.tensor.transpose(turned[:, e - e0, u, :], words[:, u * P : (u + 1) * P], ident[:])
-            dst = h_cols[:, e0 * 4 * C : e1 * 4 * C].bitcast(F32).rearrange("p (e s u) -> p e s u", e=g, u=2)
-            src = turned.rearrange("p e u s -> p e s u")
-            if gi in VECTOR_COPY_PAIRS:
-                nc.vector.tensor_copy(dst, src)
-            else:
-                nc.scalar.copy(dst, src)
+                    nc.tensor.transpose(turned[g][:, e - e0, u, :], words[:, u * P : (u + 1) * P], ident[:])
 
-        y_banks = {}
+        def unload(g, copy):
+            e0, e1 = groups[g]
+            h_cols[g] = keep.tile([P, (e1 - e0) * 4 * C], BF16, name="h_cols%d" % g, align_bytes=64)
+            copy(h_cols[g][:].bitcast(F32).rearrange("p (e s u) -> p e s u", s=C, u=2), turned[g].rearrange("p e u s -> p e s u"))
 
-        def quantise(e0, e1):
-            cols = slice(e0 * C, e1 * C)
-            nc.vector.quantize_mx(h_codes[:, cols].bitcast(FP8X4), h_scales[:, cols], h_cols[:, e0 * 4 * C : e1 * 4 * C])
-
-        def layer2(e0, e1):
+        def quantise(g):
+            e0, e1 = groups[g]
+            name = "h_rows%d" % (groups[g + 1][1] - 1) if g + 1 < VECTOR_GROUPS else "h_codes%d" % g
+            codes = keep.tile([P, (e1 - e0) * C], U32, name=name, align_bytes=64)
+            nc.vector.quantize_mx(codes[:].bitcast(FP8X4), h_scales[:, e0 * C : e1 * C], h_cols[g][:])
             for e in range(e0, e1):
-                yi, (y0, y1) = [(i, sp) for i, sp in enumerate(spans(Y_GROUPS)) if sp[0] <= e < sp[1]][0]
-                if e == y0:
-                    y_banks[yi] = bank(Y_BANKS[yi])
-                acc = y_banks[yi][:, : (y1 - y0) * C]
+                h_codes[e] = codes[:, (e - e0) * C : (e - e0 + 1) * C]
+
+        def layer2(e0, e1, b, copy):
+            acc = bank(b)[:, : (e1 - e0) * C]
+            for e in range(e0, e1):
                 cols = slice(e * C, (e + 1) * C)
                 nc.tensor.matmul_mx(
-                    acc[:, (e - y0) * C : (e - y0 + 1) * C], w2[:, e, :].bitcast(FP4X4), w2s[:, e, :],
-                    h_codes[:, cols].bitcast(FP8X4), h_scales[:, cols], start=True, stop=True,
+                    acc[:, (e - e0) * C : (e - e0 + 1) * C], w2[:, e, :].bitcast(FP4X4), w2s[:, e, :],
+                    h_codes[e].bitcast(FP8X4), h_scales[:, cols], start=True, stop=True,
                 )
-                if e + 1 == y1:
-                    if yi in VECTOR_Y_GROUPS:
-                        nc.vector.tensor_copy(y[:, y0 * C : y1 * C], acc)
-                    else:
-                        nc.scalar.copy(y[:, y0 * C : y1 * C], acc)
+            copy(y[:, e0 * C : e1 * C], acc)
 
-        done = 0
-        for a, b in spans(GATHER_CUTS):
-            gather(a, b)
-            while (done + 1) * C <= b:
-                layer1(done)
-                done += 1
-        for gi, (t0, t1) in enumerate(spans(TURN_GROUPS)):
-            turn(gi, t0, t1)
-            for e0, e1 in spans(QUANT_GROUPS):
-                if t0 < e1 <= t1:
-                    quantise(e0, e1)
-        for e0, e1 in spans(QUANT_GROUPS):
-            layer2(e0, e1)
+        code_spans = spans(CODE_CUTS)
+        for g in range(PAIRS):
+            gather(slot_scales, x_scales, 2 * g * C, 2 * (g + 1) * C)
+            if g == 0:
+                gather(slot_codes, x_codes, *code_spans[0])
+            gather(slot_codes, x_codes, *code_spans[g + 1])
+        for g in range(PAIRS):
+            layer1(2 * g)
+            layer1(2 * g + 1)
+            if g >= TURN_LAG:
+                turn(g - TURN_LAG)
+        for g in range(PAIRS - TURN_LAG, len(groups)):
+            turn(g)
+        for g in range(len(groups)):
+            unload(g, nc.vector.tensor_copy if g < VECTOR_GROUPS else nc.scalar.copy)
+            if g:
+                quantise(g - 1)
+        quantise(len(groups) - 1)
+        layer2(0, 4, 3, nc.scalar.copy)
+        layer2(4, 8, 0, nc.scalar.copy)
+        layer2(8, 10, 4, nc.vector.tensor_copy)
+        layer2(10, 11, 5, nc.scalar.copy)
+        layer2(11, 12, 6, nc.vector.tensor_copy)
 
-        for n, (a, b) in enumerate(spans(OUT_CHUNKS)):
-            w = b - a
-            prods = []
-            for r in range(3):
-                prod = keep.tile([P, w], F32, name="prod%d_%d" % (n, r), align_bytes=64)
-                nc.vector.tensor_tensor(prod[:], y[:].indirect(pos_sb[r][:, a // 16 : b // 16]), gate_sb[a // 512][:, r, a % 512 : a % 512 + w], MULT)
-                prods.append(prod)
-            res = keep.tile([P, w], F32, name="res%d" % n, align_bytes=64)
-            if n in PE_SUM_CHUNKS:
-                blocks = [slice(k * P, (k + 1) * P) for k in range(w // P)]
-                summed = [bank((a // P + k) % 6)[:, :P] for k in range(w // P)]
-                for r in range(3):
-                    for k, cols in enumerate(blocks):
-                        nc.tensor.matmul(summed[k], prods[r][:, cols], ident[:], start=(r == 0), stop=(r == 2), is_transpose=True)
-                flipped = keep.tile([P, w], F32, name="flipped%d" % n, align_bytes=64)
-                back = bank(6 + n % 2)[:, :w]
-                for k, cols in enumerate(blocks):
-                    nc.scalar.copy(flipped[:, cols], summed[k])
-                    nc.tensor.transpose(back[:, cols], flipped[:, cols], ident[:])
-                nc.scalar.copy(res[:], back)
-                nc.scalar.dma_start(out[:, a:b], res[:])
-            else:
-                part = keep.tile([P, w], F32, name="part%d" % n, align_bytes=64)
-                nc.vector.tensor_tensor(part[:], prods[0][:], prods[1][:], ADD)
-                nc.vector.tensor_tensor(res[:], part[:], prods[2][:], ADD)
-                nc.sync.dma_start(out[:, a:b], res[:])
+        prods = [keep.tile([P, T], F32, name="prod%d" % r, align_bytes=64) for r in range(3)]
+        flipped = keep.tile([P, T], F32, name="flipped", align_bytes=64)
+        res = keep.tile([P, T], F32, name="res", align_bytes=64)
+
+        def product(r, a, b):
+            nc.vector.tensor_tensor(prods[r][:, a:b], y[:].indirect(pos_sb[r][:, a // 16 : b // 16]), gate_sb[a // (T // 2)][:, r, a % (T // 2) : a % (T // 2) + b - a], MULT)
+
+        summed = {}
+
+        def add_turned(r, a, b):
+            for k in range(a // P, b // P):
+                if r == 0:
+                    summed[k] = bank(k % SUM_RING)[:, :P]
+                nc.tensor.matmul(summed[k], prods[r][:, k * P : (k + 1) * P], ident[:], start=(r == 0), stop=(r == 2), is_transpose=True)
+
+        def turn_back(a, b, bk):
+            back = bank(bk)[:, : b - a]
+            for k in range(a // P, b // P):
+                cols = slice(k * P, (k + 1) * P)
+                nc.scalar.copy(flipped[:, cols], summed[k])
+                nc.tensor.transpose(back[:, k * P - a : (k + 1) * P - a], flipped[:, cols], ident[:])
+            nc.scalar.copy(res[:, a:b], back)
+            nc.scalar.dma_start(out[:, a:b], res[:, a:b])
+
+        start, stores = 0, 0
+        for cuts in SUMMED:
+            stop = start + sum(cuts)
+            for r in range(2):
+                product(r, start, stop)
+                add_turned(r, start, stop)
+            for a, b in spans(cuts):
+                a, b = start + a, start + b
+                product(2, a, b)
+                add_turned(2, a, b)
+                for a0 in range(a, b, BANK):
+                    turn_back(a0, min(a0 + BANK, b), SUM_RING + stores % 2)
+                    stores += 1
+            start = stop
+        part = keep.tile([P, T - start], F32, name="part", align_bytes=64)
+        product(0, start, T)
+        product(1, start, T)
+        nc.vector.tensor_tensor(part[:], prods[0][:, start:], prods[1][:, start:], ADD)
+        for a in range(start, T, P):
+            product(2, a, a + P)
+        for a in range(start, T, P):
+            nc.vector.tensor_tensor(res[:, a : a + P], part[:, a - start : a - start + P], prods[2][:, a : a + P], ADD)
+            nc.sync.dma_start(out[:, a : a + P], res[:, a : a + P])

@@ -31,8 +31,10 @@ GROUPS = [2, 2, 2, 2, 2, 1, 1]
 VECTOR_GROUPS = 4
 A_RING = 4
 TURN_LAG = 2
-SUMMED = [[768], [384, 128]]
+SUMMED = [[512], [256, 256]]
+LAST_CUTS = [384, 128]
 SUM_RING = 6
+GATE_SPAN = 512
 
 
 def spans(widths):
@@ -69,7 +71,7 @@ def tile_moe_ecr_mlp_silu_kernel(
         h_rows = [keep.tile([P, H], BF16, name="h_rows%d" % e, align_bytes=64) for e in range(E)]
         h_scales = keep.tile([P, S], U8, name="h_scales", align_bytes=64)
         y = keep.tile([P, S + PAD], F32, name="y", align_bytes=64)
-        gate_sb = [keep.tile([P, 3, T // 2], F32, name="gate_sb%d" % n, align_bytes=64) for n in range(2)]
+        gate_sb = [keep.tile([P, 3, GATE_SPAN], F32, name="gate_sb%d" % n, align_bytes=64) for n in range(T // GATE_SPAN)]
         zeros = keep.tile([P, PAD], F32, name="zeros")
         ident = keep.tile([P, P], F32, name="ident", align_bytes=64)
 
@@ -114,8 +116,8 @@ def tile_moe_ecr_mlp_silu_kernel(
         load_words(w2, w2_words, 0, 12)
         nc.sync.dma_start(pos_sb[1][:], pos2)
         nc.sync.dma_start(pos_sb[2][:], pos3)
-        for n in range(2):
-            nc.sync.dma_start(gate_sb[n][:], gate.rearrange("r p t -> p r t")[:, :, n * T // 2 : (n + 1) * T // 2])
+        for n in range(T // GATE_SPAN):
+            nc.sync.dma_start(gate_sb[n][:], gate.rearrange("r p t -> p r t")[:, :, n * GATE_SPAN : (n + 1) * GATE_SPAN])
 
         for n, (a, b) in enumerate(spans(X_CHUNKS)):
             for q0, q1 in spans(X_QUANT[n]):
@@ -207,7 +209,7 @@ def tile_moe_ecr_mlp_silu_kernel(
         res = keep.tile([P, T], F32, name="res", align_bytes=64)
 
         def product(r, a, b):
-            nc.vector.tensor_tensor(prods[r][:, a:b], y[:].indirect(pos_sb[r][:, a // 16 : b // 16]), gate_sb[a // (T // 2)][:, r, a % (T // 2) : a % (T // 2) + b - a], MULT)
+            nc.vector.tensor_tensor(prods[r][:, a:b], y[:].indirect(pos_sb[r][:, a // 16 : b // 16]), gate_sb[a // (GATE_SPAN)][:, r, a % (GATE_SPAN) : a % (GATE_SPAN) + b - a], MULT)
 
         summed = {}
 
@@ -244,8 +246,8 @@ def tile_moe_ecr_mlp_silu_kernel(
         product(0, start, T)
         product(1, start, T)
         nc.vector.tensor_tensor(part[:], prods[0][:, start:], prods[1][:, start:], ADD)
-        for a in range(start, T, P):
-            product(2, a, a + P)
-        for a in range(start, T, P):
-            nc.vector.tensor_tensor(res[:, a : a + P], part[:, a - start : a - start + P], prods[2][:, a : a + P], ADD)
-            nc.sync.dma_start(out[:, a : a + P], res[:, a : a + P])
+        for a, b in spans(LAST_CUTS):
+            product(2, start + a, start + b)
+        for a, b in spans(LAST_CUTS):
+            nc.vector.tensor_tensor(res[:, start + a : start + b], part[:, a:b], prods[2][:, start + a : start + b], ADD)
+            nc.sync.dma_start(out[:, start + a : start + b], res[:, start + a : start + b])

@@ -22,8 +22,8 @@ SILU = mybir.ActivationFunctionType.Silu
 MULT = mybir.AluOpType.mult
 ADD = mybir.AluOpType.add
 
-X_CHUNKS = [512,512,256,128,128]
-X_QUANT = [[512],[256,256],[256],[128],[128]]
+X_CHUNKS = [512,384,256,256,128]
+X_QUANT = [[512],[256,128],[256],[256],[128]]
 SCALAR_SHARE = {128:64,256:128,512:256}
 PAIRS = E // 2
 CODE_CUTS = [192, 192, 256, 256, 256, 192, 192]
@@ -32,7 +32,7 @@ VECTOR_GROUPS = 4
 A_RING = 4
 TURN_LAG = 2
 SUMMED = [[512], [256, 256]]
-LAST_CUTS = [384, 128]
+LAST = 128
 SUM_RING = 6
 GATE_SPAN = 512
 
@@ -243,11 +243,21 @@ def tile_moe_ecr_mlp_silu_kernel(
                     stores += 1
             start = stop
         part = keep.tile([P, T - start], F32, name="part", align_bytes=64)
-        product(0, start, T)
-        product(1, start, T)
-        nc.vector.tensor_tensor(part[:], prods[0][:, start:], prods[1][:, start:], ADD)
-        for a, b in spans(LAST_CUTS):
-            product(2, start + a, start + b)
-        for a, b in spans(LAST_CUTS):
-            nc.vector.tensor_tensor(res[:, start + a : start + b], part[:, a:b], prods[2][:, start + a : start + b], ADD)
-            nc.sync.dma_start(out[:, start + a : start + b], res[:, start + a : start + b])
+
+        def add_first_two(a, b):
+            nc.vector.tensor_tensor(part[:, a - start : b - start], prods[0][:, a:b], prods[1][:, a:b], ADD)
+
+        def add_third(a, b):
+            nc.vector.tensor_tensor(res[:, a:b], part[:, a - start : b - start], prods[2][:, a:b], ADD)
+            nc.sync.dma_start(out[:, a:b], res[:, a:b])
+
+        last = T - LAST
+        for r in range(3):
+            product(r, start, last)
+        add_first_two(start, last)
+        product(0, last, T)
+        add_third(start, last)
+        product(1, last, T)
+        product(2, last, T)
+        add_first_two(last, T)
+        add_third(last, T)

@@ -102,13 +102,13 @@ def tile_moe_ecr_mlp_silu_kernel(
                 nc.sync.dma_start(dst[r:P:32, e0:e1, :].bitcast(I32), rows[r][:, e0:e1, :])
 
         load_x(0)
-        nc.sync.dma_start(offs_sb[:], offs)
-        nc.sync.dma_start(pos_sb[0][:], pos1)
         load_x(1)
         load_x(2)
         load_x(3)
         load_x(4)
+        nc.sync.dma_start(offs_sb[:], offs)
         load_words(w1, w1_words, 0, 2)
+        nc.sync.dma_start(pos_sb[0][:], pos1)
         load_scales(w1s, w1_scales, 0, 12)
         load_words(w1, w1_words, 2, 6)
         load_words(w1, w1_words, 6, 12)
@@ -151,7 +151,7 @@ def tile_moe_ecr_mlp_silu_kernel(
 
         def turn(g):
             e0, e1 = groups[g]
-            turned[g] = bank((A_RING + g) % 8)[:, : (e1 - e0) * 2 * C].rearrange("p (e u s) -> p e u s", u=2, s=C)
+            turned[g] = bank(A_RING + g if g < A_RING else (e1 - 1) % A_RING if e1 - e0 == 1 else 0)[:, : (e1 - e0) * 2 * C].rearrange("p (e u s) -> p e u s", u=2, s=C)
             for e in range(e0, e1):
                 words = h_rows[e][:].bitcast(F32)
                 for u in range(2):
@@ -198,8 +198,9 @@ def tile_moe_ecr_mlp_silu_kernel(
             if g:
                 quantise(g - 1)
         quantise(len(groups) - 1)
-        layer2(0, 4, 3, nc.scalar.copy)
-        layer2(4, 8, 0, nc.scalar.copy)
+        layer2(0, 2, 1, nc.scalar.copy)
+        layer2(2, 6, 0, nc.scalar.copy)
+        layer2(6, 8, 2, nc.vector.tensor_copy)
         layer2(8, 10, 4, nc.vector.tensor_copy)
         layer2(10, 11, 5, nc.scalar.copy)
         layer2(11, 12, 6, nc.vector.tensor_copy)

@@ -22,11 +22,12 @@ SILU = mybir.ActivationFunctionType.Silu
 MULT = mybir.AluOpType.mult
 ADD = mybir.AluOpType.add
 
-X_CHUNKS = [512,384,256,256,128]
-X_QUANT = [[512],[256,128],[256],[256],[128]]
+X_CHUNKS = [640, 512, 256, 128]
+X_QUANT = [[512, 128], [256, 256], [256], [128]]
 SCALAR_SHARE = {128:64,256:128,512:256}
 PAIRS = E // 2
-CODE_CUTS = [192, 192, 256, 256, 256, 192, 192]
+SCALE_CUTS = [256, 384, 384, 256, 256]
+CODE_CUTS = [192, 192, 384, 384, 384]
 GROUPS = [2, 2, 2, 2, 2, 1, 1]
 VECTOR_GROUPS = 4
 A_RING = 4
@@ -105,9 +106,9 @@ def tile_moe_ecr_mlp_silu_kernel(
         load_x(1)
         load_x(2)
         load_x(3)
-        load_x(4)
         nc.sync.dma_start(offs_sb[:], offs)
-        load_words(w1, w1_words, 0, 2)
+        load_words(w1, w1_words, 0, 1)
+        load_words(w1, w1_words, 1, 2)
         nc.sync.dma_start(pos_sb[0][:], pos1)
         load_scales(w1s, w1_scales, 0, 12)
         load_words(w1, w1_words, 2, 6)
@@ -181,11 +182,12 @@ def tile_moe_ecr_mlp_silu_kernel(
             copy(y[:, e0 * C : e1 * C], acc)
 
         code_spans = spans(CODE_CUTS)
-        for g in range(PAIRS):
-            gather(slot_scales, x_scales, 2 * g * C, 2 * (g + 1) * C)
+        for g, cut in enumerate(spans(SCALE_CUTS)):
+            gather(slot_scales, x_scales, *cut)
             if g == 0:
                 gather(slot_codes, x_codes, *code_spans[0])
-            gather(slot_codes, x_codes, *code_spans[g + 1])
+            if g + 1 < len(code_spans):
+                gather(slot_codes, x_codes, *code_spans[g + 1])
         for g in range(PAIRS):
             layer1(2 * g)
             layer1(2 * g + 1)

@@ -26,11 +26,13 @@ X_CHUNKS = [640, 512, 256, 128]
 X_QUANT = [[512, 128], [256, 256], [256], [128]]
 SCALAR_SHARE = {128:64,256:128,512:256}
 PAIRS = E // 2
+SCALE_RUNS = [8, 4]
 SCALE_CUTS = [256, 384, 384, 256, 256]
 CODE_CUTS = [192, 192, 384, 384, 384]
 GROUPS = [2, 2, 2, 2, 2, 1, 1]
 VECTOR_GROUPS = 4
 A_RING = 4
+TURN_BANKS = [4, 5, 6, 0, 7, 2, 3]
 TURN_LAG = 2
 SUMMED = [[512], [256, 256]]
 LAST = 128
@@ -66,7 +68,8 @@ def tile_moe_ecr_mlp_silu_kernel(
         slot_codes = keep.tile([P, S], U32, name="slot_codes", align_bytes=64)
         slot_scales = keep.tile([P, S], U8, name="slot_scales", align_bytes=64)
         w1 = keep.tile([P, E, 2 * H], U8, name="w1", align_bytes=64)
-        w1s = keep.tile([P, E, H], U8, name="w1s", align_bytes=64)
+        w1s_runs = [keep.tile([P, b - a, H], U8, name="w1s%d" % a, align_bytes=64) for a, b in spans(SCALE_RUNS)]
+        w1s = [run[:, e, :] for run, n in zip(w1s_runs, SCALE_RUNS) for e in range(n)]
         w2 = keep.tile([P, E, 2 * N], U8, name="w2", align_bytes=64)
         w2s = keep.tile([P, E, N], U8, name="w2s", align_bytes=64)
         h_rows = [keep.tile([P, H], BF16, name="h_rows%d" % e, align_bytes=64) for e in range(E)]
@@ -78,7 +81,8 @@ def tile_moe_ecr_mlp_silu_kernel(
 
         nc.vector.memset(zeros[:], 0.0)
         nc.scalar.activation(y[:, S:], zeros[:], SILU)
-        nc.vector.memset(w1s[:].rearrange("p e c -> p (e c)").bitcast(I32), 0)
+        for run in w1s_runs:
+            nc.vector.memset(run[:].rearrange("p e c -> p (e c)").bitcast(I32), 0)
         nc.vector.memset(w2s[:].rearrange("p e c -> p (e c)").bitcast(I32), 0)
         nc.vector.memset(x_scales[:].bitcast(I32), 0)
         make_identity(nc, ident[:])
@@ -100,7 +104,7 @@ def tile_moe_ecr_mlp_silu_kernel(
         def load_scales(dst, src, e0, e1):
             rows = src.bitcast(I32).rearrange("e s (q r) c -> r q (e s) c", r=4)
             for r in range(4):
-                nc.sync.dma_start(dst[r:P:32, e0:e1, :].bitcast(I32), rows[r][:, e0:e1, :])
+                nc.sync.dma_start(dst[r:P:32, :, :].bitcast(I32), rows[r][:, e0:e1, :])
 
         load_x(0)
         load_x(1)
@@ -110,9 +114,10 @@ def tile_moe_ecr_mlp_silu_kernel(
         load_words(w1, w1_words, 0, 1)
         load_words(w1, w1_words, 1, 2)
         nc.sync.dma_start(pos_sb[0][:], pos1)
-        load_scales(w1s, w1_scales, 0, 12)
+        load_scales(w1s_runs[0], w1_scales, 0, 8)
         load_words(w1, w1_words, 2, 6)
         load_words(w1, w1_words, 6, 12)
+        load_scales(w1s_runs[1], w1_scales, 8, 12)
         load_scales(w2s, w2_scales, 0, 12)
         load_words(w2, w2_words, 0, 12)
         nc.sync.dma_start(pos_sb[1][:], pos2)
@@ -143,7 +148,7 @@ def tile_moe_ecr_mlp_silu_kernel(
             acc = bank(e % A_RING)[:]
             nc.tensor.matmul_mx(
                 acc, slot_codes[:, cols].bitcast(FP8X4), slot_scales[:, cols],
-                w1[:, e, :].bitcast(FP4X4), w1s[:, e, :], start=True, stop=True,
+                w1[:, e, :].bitcast(FP4X4), w1s[e], start=True, stop=True,
             )
             nc.scalar.activation(h_rows[e][:].rearrange("s (u p d) -> s u p d", u=2, d=2), acc.rearrange("s (p u d) -> s u p d", u=2, d=2), SILU)
 
@@ -152,7 +157,7 @@ def tile_moe_ecr_mlp_silu_kernel(
 
         def turn(g):
             e0, e1 = groups[g]
-            turned[g] = bank(A_RING + g if g < A_RING else (e1 - 1) % A_RING if e1 - e0 == 1 else 0)[:, : (e1 - e0) * 2 * C].rearrange("p (e u s) -> p e u s", u=2, s=C)
+            turned[g] = bank(TURN_BANKS[g])[:, : (e1 - e0) * 2 * C].rearrange("p (e u s) -> p e u s", u=2, s=C)
             for e in range(e0, e1):
                 words = h_rows[e][:].bitcast(F32)
                 for u in range(2):
@@ -201,11 +206,11 @@ def tile_moe_ecr_mlp_silu_kernel(
                 quantise(g - 1)
         quantise(len(groups) - 1)
         layer2(0, 2, 1, nc.scalar.copy)
-        layer2(2, 6, 0, nc.scalar.copy)
-        layer2(6, 8, 2, nc.vector.tensor_copy)
+        layer2(2, 6, 6, nc.scalar.copy)
+        layer2(6, 8, 0, nc.vector.tensor_copy)
         layer2(8, 10, 4, nc.vector.tensor_copy)
         layer2(10, 11, 5, nc.scalar.copy)
-        layer2(11, 12, 6, nc.vector.tensor_copy)
+        layer2(11, 12, 7, nc.vector.tensor_copy)
 
         prods = [keep.tile([P, T], F32, name="prod%d" % r, align_bytes=64) for r in range(3)]
         flipped = keep.tile([P, T], F32, name="flipped", align_bytes=64)

@@ -22,18 +22,15 @@ SILU = mybir.ActivationFunctionType.Silu
 MULT = mybir.AluOpType.mult
 ADD = mybir.AluOpType.add
 
-X_CHUNKS = [640, 512, 256, 128]
-X_QUANT = [[512, 128], [256, 256], [256], [128]]
-SCALAR_SHARE = {128:64,256:128,512:256}
-PAIRS = E // 2
+X_LOADS = [[512, 128], [256, 256], [256], [128]]
 SCALE_RUNS = [8, 4]
 SCALE_CUTS = [256, 384, 384, 256, 256]
-CODE_CUTS = [192, 192, 384, 384, 384]
+WORD_CUTS = [192, 192, 384, 384, 384]
 GROUPS = [2, 2, 2, 2, 2, 1, 1]
 VECTOR_GROUPS = 4
-A_RING = 4
-TURN_BANKS = [4, 5, 6, 0, 7, 2, 3]
+RING = 4
 TURN_LAG = 2
+TURN_BANKS = [4, 5, 6, 8 % RING, 7, 10 % RING, 11 % RING]
 SUMMED = [[512], [256, 256]]
 LAST = 128
 SUM_RING = 6
@@ -41,11 +38,11 @@ GATE_SPAN = 512
 
 
 def spans(widths):
-    out, a = [], 0
-    for w in widths:
-        out.append((a, a + w))
-        a += w
-    return out
+    pairs, start = [], 0
+    for width in widths:
+        pairs.append((start, start + width))
+        start += width
+    return pairs
 
 
 def tile_moe_ecr_mlp_silu_kernel(
@@ -68,8 +65,8 @@ def tile_moe_ecr_mlp_silu_kernel(
         slot_codes = keep.tile([P, S], U32, name="slot_codes", align_bytes=64)
         slot_scales = keep.tile([P, S], U8, name="slot_scales", align_bytes=64)
         w1 = keep.tile([P, E, 2 * H], U8, name="w1", align_bytes=64)
-        w1s_runs = [keep.tile([P, b - a, H], U8, name="w1s%d" % a, align_bytes=64) for a, b in spans(SCALE_RUNS)]
-        w1s = [run[:, e, :] for run, n in zip(w1s_runs, SCALE_RUNS) for e in range(n)]
+        w1s_runs = [keep.tile([P, e1 - e0, H], U8, name="w1s%d" % e0, align_bytes=64) for e0, e1 in spans(SCALE_RUNS)]
+        w1s = [run[:, e, :] for run, count in zip(w1s_runs, SCALE_RUNS) for e in range(count)]
         w2 = keep.tile([P, E, 2 * N], U8, name="w2", align_bytes=64)
         w2s = keep.tile([P, E, N], U8, name="w2s", align_bytes=64)
         h_rows = [keep.tile([P, H], BF16, name="h_rows%d" % e, align_bytes=64) for e in range(E)]
@@ -87,14 +84,6 @@ def tile_moe_ecr_mlp_silu_kernel(
         nc.vector.memset(x_scales[:].bitcast(I32), 0)
         make_identity(nc, ident[:])
 
-        x_rows = xT.rearrange("(p j) t -> p j t", j=4)
-        x_raw = {}
-
-        def load_x(n):
-            a, b = spans(X_CHUNKS)[n]
-            x_raw[n] = keep.tile([P, 4, b - a], F32, name="x_raw%d" % n, align_bytes=64)
-            nc.sync.dma_start(x_raw[n][:], x_rows[:, :, a:b])
-
         def load_words(dst, src, e0, e1):
             nc.sync.dma_start(
                 dst[:, e0:e1, :].bitcast(I32),
@@ -106,36 +95,36 @@ def tile_moe_ecr_mlp_silu_kernel(
             for r in range(4):
                 nc.sync.dma_start(dst[r:P:32, :, :].bitcast(I32), rows[r][:, e0:e1, :])
 
-        load_x(0)
-        load_x(1)
-        load_x(2)
-        load_x(3)
+        x_rows = xT.rearrange("(p j) t -> p j t", j=4)
+        x_spans = spans([sum(pieces) for pieces in X_LOADS])
+        x_raw = []
+        for n, (a, b) in enumerate(x_spans):
+            x_raw.append(keep.tile([P, 4, b - a], F32, name="x_raw%d" % n, align_bytes=64))
+            nc.sync.dma_start(x_raw[n][:], x_rows[:, :, a:b])
         nc.sync.dma_start(offs_sb[:], offs)
         load_words(w1, w1_words, 0, 1)
         load_words(w1, w1_words, 1, 2)
         nc.sync.dma_start(pos_sb[0][:], pos1)
-        load_scales(w1s_runs[0], w1_scales, 0, 8)
-        load_words(w1, w1_words, 2, 6)
-        load_words(w1, w1_words, 6, 12)
-        load_scales(w1s_runs[1], w1_scales, 8, 12)
-        load_scales(w2s, w2_scales, 0, 12)
-        load_words(w2, w2_words, 0, 12)
+        (first_run, second_run), half = spans(SCALE_RUNS), E // 2
+        load_scales(w1s_runs[0], w1_scales, *first_run)
+        load_words(w1, w1_words, 2, half)
+        load_words(w1, w1_words, half, E)
+        load_scales(w1s_runs[1], w1_scales, *second_run)
+        load_scales(w2s, w2_scales, 0, E)
+        load_words(w2, w2_words, 0, E)
         nc.sync.dma_start(pos_sb[1][:], pos2)
         nc.sync.dma_start(pos_sb[2][:], pos3)
         for n in range(T // GATE_SPAN):
             nc.sync.dma_start(gate_sb[n][:], gate.rearrange("r p t -> p r t")[:, :, n * GATE_SPAN : (n + 1) * GATE_SPAN])
 
-        for n, (a, b) in enumerate(spans(X_CHUNKS)):
-            for q0, q1 in spans(X_QUANT[n]):
-                w = q1 - q0
-                cut = w - SCALAR_SHARE[w]
-                xb = keep.tile([P, w, 4], BF16, name="xb%d" % (a + q0), align_bytes=64)
+        for n, (a, b) in enumerate(x_spans):
+            for q0, q1 in spans(X_LOADS[n]):
+                quads = (q1 - q0) // 4
+                xb = keep.tile([P, q1 - q0, 4], BF16, name="xb%d" % (a + q0), align_bytes=64)
                 dst = xb[:].rearrange("p (c i) j -> p c j i", i=4)
                 src = x_raw[n][:, :, q0:q1].rearrange("p j (c i) -> p c j i", i=4)
-                if cut:
-                    nc.vector.tensor_copy(dst[:, : cut // 4], src[:, : cut // 4])
-                if cut < w:
-                    nc.scalar.copy(dst[:, cut // 4 :], src[:, cut // 4 :])
+                nc.vector.tensor_copy(dst[:, : quads // 2], src[:, : quads // 2])
+                nc.scalar.copy(dst[:, quads // 2 :], src[:, quads // 2 :])
                 nc.vector.quantize_mx(
                     x_codes[:, a + q0 : a + q1].bitcast(FP8X4), x_scales[:, a + q0 : a + q1], xb[:].rearrange("p t j -> p (t j)")
                 )
@@ -145,7 +134,7 @@ def tile_moe_ecr_mlp_silu_kernel(
 
         def layer1(e):
             cols = slice(e * C, (e + 1) * C)
-            acc = bank(e % A_RING)[:]
+            acc = bank(e % RING)[:]
             nc.tensor.matmul_mx(
                 acc, slot_codes[:, cols].bitcast(FP8X4), slot_scales[:, cols],
                 w1[:, e, :].bitcast(FP4X4), w1s[e], start=True, stop=True,
@@ -159,9 +148,9 @@ def tile_moe_ecr_mlp_silu_kernel(
             e0, e1 = groups[g]
             turned[g] = bank(TURN_BANKS[g])[:, : (e1 - e0) * 2 * C].rearrange("p (e u s) -> p e u s", u=2, s=C)
             for e in range(e0, e1):
-                words = h_rows[e][:].bitcast(F32)
+                units = h_rows[e][:].bitcast(F32)
                 for u in range(2):
-                    nc.tensor.transpose(turned[g][:, e - e0, u, :], words[:, u * P : (u + 1) * P], ident[:])
+                    nc.tensor.transpose(turned[g][:, e - e0, u, :], units[:, u * P : (u + 1) * P], ident[:])
 
         def unload(g, copy):
             e0, e1 = groups[g]
@@ -186,69 +175,67 @@ def tile_moe_ecr_mlp_silu_kernel(
                 )
             copy(y[:, e0 * C : e1 * C], acc)
 
-        code_spans = spans(CODE_CUTS)
-        for g, cut in enumerate(spans(SCALE_CUTS)):
-            gather(slot_scales, x_scales, *cut)
-            if g == 0:
-                gather(slot_codes, x_codes, *code_spans[0])
-            if g + 1 < len(code_spans):
-                gather(slot_codes, x_codes, *code_spans[g + 1])
-        for g in range(PAIRS):
-            layer1(2 * g)
-            layer1(2 * g + 1)
-            if g >= TURN_LAG:
-                turn(g - TURN_LAG)
-        for g in range(PAIRS - TURN_LAG, len(groups)):
+        scale_spans, word_spans = spans(SCALE_CUTS), spans(WORD_CUTS)
+        gather(slot_scales, x_scales, *scale_spans[0])
+        gather(slot_codes, x_codes, *word_spans[0])
+        for word_span, scale_span in zip(word_spans[1:], scale_spans[1:]):
+            gather(slot_codes, x_codes, *word_span)
+            gather(slot_scales, x_scales, *scale_span)
+        for pair in range(E // 2):
+            layer1(2 * pair)
+            layer1(2 * pair + 1)
+            if pair >= TURN_LAG:
+                turn(pair - TURN_LAG)
+        for g in range(E // 2 - TURN_LAG, len(groups)):
             turn(g)
         for g in range(len(groups)):
             unload(g, nc.vector.tensor_copy if g < VECTOR_GROUPS else nc.scalar.copy)
             if g:
                 quantise(g - 1)
         quantise(len(groups) - 1)
-        layer2(0, 2, 1, nc.scalar.copy)
-        layer2(2, 6, 6, nc.scalar.copy)
-        layer2(6, 8, 0, nc.vector.tensor_copy)
-        layer2(8, 10, 4, nc.vector.tensor_copy)
-        layer2(10, 11, 5, nc.scalar.copy)
-        layer2(11, 12, 7, nc.vector.tensor_copy)
+        layer2(0, 2, 9 % RING, nc.scalar.copy)
+        layer2(2, 6, TURN_BANKS[2], nc.scalar.copy)
+        layer2(6, 8, TURN_BANKS[3], nc.vector.tensor_copy)
+        layer2(8, 10, TURN_BANKS[0], nc.vector.tensor_copy)
+        layer2(10, 11, TURN_BANKS[1], nc.scalar.copy)
+        layer2(11, 12, TURN_BANKS[4], nc.scalar.copy)
 
         prods = [keep.tile([P, T], F32, name="prod%d" % r, align_bytes=64) for r in range(3)]
         flipped = keep.tile([P, T], F32, name="flipped", align_bytes=64)
         res = keep.tile([P, T], F32, name="res", align_bytes=64)
 
         def product(r, a, b):
-            nc.vector.tensor_tensor(prods[r][:, a:b], y[:].indirect(pos_sb[r][:, a // 16 : b // 16]), gate_sb[a // (GATE_SPAN)][:, r, a % (GATE_SPAN) : a % (GATE_SPAN) + b - a], MULT)
+            n, g0 = divmod(a, GATE_SPAN)
+            nc.vector.tensor_tensor(prods[r][:, a:b], y[:].indirect(pos_sb[r][:, a // 16 : b // 16]), gate_sb[n][:, r, g0 : g0 + b - a], MULT)
 
         summed = {}
 
         def add_turned(r, a, b):
-            for k in range(a // P, b // P):
+            for blk in range(a // P, b // P):
                 if r == 0:
-                    summed[k] = bank(k % SUM_RING)[:, :P]
-                nc.tensor.matmul(summed[k], prods[r][:, k * P : (k + 1) * P], ident[:], start=(r == 0), stop=(r == 2), is_transpose=True)
+                    summed[blk] = bank(blk % SUM_RING)[:, :P]
+                nc.tensor.matmul(summed[blk], prods[r][:, blk * P : (blk + 1) * P], ident[:], start=(r == 0), stop=(r == 2), is_transpose=True)
 
-        def turn_back(a, b, bk):
-            back = bank(bk)[:, : b - a]
-            for k in range(a // P, b // P):
-                cols = slice(k * P, (k + 1) * P)
-                nc.scalar.copy(flipped[:, cols], summed[k])
-                nc.tensor.transpose(back[:, k * P - a : (k + 1) * P - a], flipped[:, cols], ident[:])
+        def turn_back(a, b, back_bank):
+            back = bank(back_bank)[:, : b - a]
+            for blk in range(a // P, b // P):
+                cols = slice(blk * P, (blk + 1) * P)
+                nc.scalar.copy(flipped[:, cols], summed[blk])
+                nc.tensor.transpose(back[:, blk * P - a : (blk + 1) * P - a], flipped[:, cols], ident[:])
             nc.scalar.copy(res[:, a:b], back)
             nc.scalar.dma_start(out[:, a:b], res[:, a:b])
 
         start, stores = 0, 0
-        for cuts in SUMMED:
-            stop = start + sum(cuts)
+        for pieces in SUMMED:
+            stop = start + sum(pieces)
             for r in range(2):
                 product(r, start, stop)
                 add_turned(r, start, stop)
-            for a, b in spans(cuts):
-                a, b = start + a, start + b
-                product(2, a, b)
-                add_turned(2, a, b)
-                for a0 in range(a, b, BANK):
-                    turn_back(a0, min(a0 + BANK, b), SUM_RING + stores % 2)
-                    stores += 1
+            for a, b in spans(pieces):
+                product(2, start + a, start + b)
+                add_turned(2, start + a, start + b)
+                turn_back(start + a, start + b, SUM_RING + stores % 2)
+                stores += 1
             start = stop
         part = keep.tile([P, T - start], F32, name="part", align_bytes=64)
 

@@ -19,6 +19,7 @@ U8 = mybir.dt.uint8
 FP8X4 = mybir.dt.float8_e4m3fn_x4
 FP4X4 = mybir.dt.float4_e2m1fn_x4
 SILU = mybir.ActivationFunctionType.Silu
+COPY = mybir.ActivationFunctionType.Copy
 MULT = mybir.AluOpType.mult
 ADD = mybir.AluOpType.add
 
@@ -31,10 +32,8 @@ VECTOR_GROUPS = 4
 RING = 4
 TURN_LAG = 2
 TURN_BANKS = [4, 5, 6, 8 % RING, 7, 10 % RING, 11 % RING]
-SUMMED = [[512], [256, 256]]
-LAST = 128
-SUM_RING = 6
-GATE_SPAN = 512
+SUMMED = [384, 384, 256]
+ADDED = [384, 128]
 
 
 def spans(widths):
@@ -72,7 +71,8 @@ def tile_moe_ecr_mlp_silu_kernel(
         h_rows = [keep.tile([P, H], BF16, name="h_rows%d" % e, align_bytes=64) for e in range(E)]
         h_scales = keep.tile([P, S], U8, name="h_scales", align_bytes=64)
         y = keep.tile([P, S + PAD], F32, name="y", align_bytes=64)
-        gate_sb = [keep.tile([P, 3, GATE_SPAN], F32, name="gate_sb%d" % n, align_bytes=64) for n in range(T // GATE_SPAN)]
+        gate_spans = spans(SUMMED + [sum(ADDED)])
+        gate_sb = [keep.tile([P, 3, b - a], F32, name="gate_sb%d" % a, align_bytes=64) for a, b in gate_spans]
         zeros = keep.tile([P, PAD], F32, name="zeros")
         ident = keep.tile([P, P], F32, name="ident", align_bytes=64)
 
@@ -114,8 +114,8 @@ def tile_moe_ecr_mlp_silu_kernel(
         load_words(w2, w2_words, 0, E)
         nc.sync.dma_start(pos_sb[1][:], pos2)
         nc.sync.dma_start(pos_sb[2][:], pos3)
-        for n in range(T // GATE_SPAN):
-            nc.sync.dma_start(gate_sb[n][:], gate.rearrange("r p t -> p r t")[:, :, n * GATE_SPAN : (n + 1) * GATE_SPAN])
+        for n, (a, b) in enumerate(gate_spans):
+            nc.sync.dma_start(gate_sb[n][:], gate.rearrange("r p t -> p r t")[:, :, a:b])
 
         for n, (a, b) in enumerate(x_spans):
             for q0, q1 in spans(X_LOADS[n]):
@@ -200,59 +200,76 @@ def tile_moe_ecr_mlp_silu_kernel(
         layer2(10, 11, TURN_BANKS[1], nc.scalar.copy)
         layer2(11, 12, TURN_BANKS[4], nc.scalar.copy)
 
+        fetched = [keep.tile([P, T], F32, name="fetched%d" % r, align_bytes=64) for r in range(2)]
         prods = [keep.tile([P, T], F32, name="prod%d" % r, align_bytes=64) for r in range(3)]
         flipped = keep.tile([P, T], F32, name="flipped", align_bytes=64)
         res = keep.tile([P, T], F32, name="res", align_bytes=64)
 
-        def product(r, a, b):
-            n, g0 = divmod(a, GATE_SPAN)
-            nc.vector.tensor_tensor(prods[r][:, a:b], y[:].indirect(pos_sb[r][:, a // 16 : b // 16]), gate_sb[n][:, r, g0 : g0 + b - a], MULT)
+        def weights(r, a, b):
+            n = max(m for m, span in enumerate(gate_spans) if span[0] <= a)
+            return gate_sb[n][:, r, a - gate_spans[n][0] : b - gate_spans[n][0]]
 
-        summed = {}
+        def named(r, a, b):
+            return y[:].indirect(pos_sb[r][:, a // 16 : b // 16])
 
-        def add_turned(r, a, b):
+        def fetch(r, a, b):
+            nc.scalar.activation(fetched[r][:, a:b], named(r, a, b), COPY)
+
+        def weigh(r, a, b):
+            nc.vector.tensor_tensor(prods[r][:, a:b], fetched[r][:, a:b], weights(r, a, b), MULT)
+
+        def fetch_weighed(r, a, b):
+            nc.vector.tensor_tensor(prods[r][:, a:b], named(r, a, b), weights(r, a, b), MULT)
+
+        def add_turned(acc, r, a, b, first, last):
+            blocks = range(a // P, b // P)
+            for blk in blocks:
+                nc.tensor.matmul(
+                    acc[:, blk * P - a : (blk + 1) * P - a], prods[r][:, blk * P : (blk + 1) * P], ident[:],
+                    start=first and blk == blocks[0], stop=last and blk == blocks[-1], is_transpose=True,
+                )
+
+        def turn_back(acc, back, a, b):
+            nc.scalar.copy(flipped[:, a:b], acc)
             for blk in range(a // P, b // P):
-                if r == 0:
-                    summed[blk] = bank(blk % SUM_RING)[:, :P]
-                nc.tensor.matmul(summed[blk], prods[r][:, blk * P : (blk + 1) * P], ident[:], start=(r == 0), stop=(r == 2), is_transpose=True)
+                nc.tensor.transpose(back[:, blk * P - a : (blk + 1) * P - a], flipped[:, blk * P : (blk + 1) * P], ident[:])
 
-        def turn_back(a, b, back_bank):
-            back = bank(back_bank)[:, : b - a]
-            for blk in range(a // P, b // P):
-                cols = slice(blk * P, (blk + 1) * P)
-                nc.scalar.copy(flipped[:, cols], summed[blk])
-                nc.tensor.transpose(back[:, blk * P - a : (blk + 1) * P - a], flipped[:, cols], ident[:])
+        def leave(back, a, b):
             nc.scalar.copy(res[:, a:b], back)
             nc.scalar.dma_start(out[:, a:b], res[:, a:b])
 
-        start, stores = 0, 0
-        for pieces in SUMMED:
-            stop = start + sum(pieces)
-            for r in range(2):
-                product(r, start, stop)
-                add_turned(r, start, stop)
-            for a, b in spans(pieces):
-                product(2, start + a, start + b)
-                add_turned(2, start + a, start + b)
-                turn_back(start + a, start + b, SUM_RING + stores % 2)
-                stores += 1
-            start = stop
+        chunks = spans(SUMMED)
+        start = sum(SUMMED)
+        last = T - ADDED[-1]
+        sums = [bank(n)[:, : b - a] for n, (a, b) in enumerate(chunks)]
+        backs = [bank(len(chunks) + n)[:, : b - a] for n, (a, b) in enumerate(chunks)]
+        for a, b in chunks:
+            fetch(0, a, b)
+        for n, (a, b) in enumerate(chunks):
+            fetch_weighed(1, a, b)
+            add_turned(sums[n], 1, a, b, True, False)
+            fetch_weighed(2, a, b)
+            add_turned(sums[n], 2, a, b, False, False)
+            weigh(0, a, b)
+            add_turned(sums[n], 0, a, b, False, True)
+        turn_back(sums[0], backs[0], *chunks[0])
+        fetch(0, start, T)
+        leave(backs[0], *chunks[0])
+        turn_back(sums[1], backs[1], *chunks[1])
+        fetch(1, start, T)
+        leave(backs[1], *chunks[1])
+        turn_back(sums[2], backs[2], *chunks[2])
+        leave(backs[2], *chunks[2])
+
         part = keep.tile([P, T - start], F32, name="part", align_bytes=64)
-
-        def add_first_two(a, b):
-            nc.vector.tensor_tensor(part[:, a - start : b - start], prods[0][:, a:b], prods[1][:, a:b], ADD)
-
-        def add_third(a, b):
-            nc.vector.tensor_tensor(res[:, a:b], part[:, a - start : b - start], prods[2][:, a:b], ADD)
-            nc.sync.dma_start(out[:, a:b], res[:, a:b])
-
-        last = T - LAST
-        for r in range(3):
-            product(r, start, last)
-        add_first_two(start, last)
-        product(0, last, T)
-        add_third(start, last)
-        product(1, last, T)
-        product(2, last, T)
-        add_first_two(last, T)
-        add_third(last, T)
+        fetch_weighed(2, start, last)
+        weigh(0, start, T)
+        weigh(1, start, last)
+        nc.vector.tensor_tensor(part[:, : last - start], prods[2][:, start:last], prods[0][:, start:last], ADD)
+        weigh(1, last, T)
+        nc.vector.tensor_tensor(res[:, start:last], part[:, : last - start], prods[1][:, start:last], ADD)
+        nc.sync.dma_start(out[:, start:last], res[:, start:last])
+        nc.vector.tensor_tensor(part[:, last - start :], prods[0][:, last:T], prods[1][:, last:T], ADD)
+        fetch_weighed(2, last, T)
+        nc.vector.tensor_tensor(res[:, last:T], part[:, last - start :], prods[2][:, last:T], ADD)
+        nc.sync.dma_start(out[:, last:T], res[:, last:T])

@@ -32,8 +32,8 @@ VECTOR_GROUPS = 4
 RING = 4
 TURN_LAG = 2
 TURN_BANKS = [4, 5, 6, 8 % RING, 7, 10 % RING, 11 % RING]
-SUMMED = [384, 384, 256]
-ADDED = [384, 128]
+TURNED = [256, 256, 256]
+DIRECT = [384, 256, 128]
 
 
 def spans(widths):
@@ -71,8 +71,12 @@ def tile_moe_ecr_mlp_silu_kernel(
         h_rows = [keep.tile([P, H], BF16, name="h_rows%d" % e, align_bytes=64) for e in range(E)]
         h_scales = keep.tile([P, S], U8, name="h_scales", align_bytes=64)
         y = keep.tile([P, S + PAD], F32, name="y", align_bytes=64)
-        gate_spans = spans(SUMMED + [sum(ADDED)])
-        gate_sb = [keep.tile([P, 3, b - a], F32, name="gate_sb%d" % a, align_bytes=64) for a, b in gate_spans]
+        turned_tokens = sum(TURNED)
+        gate_rows = keep.tile([P, P], F32, name="gate_rows", align_bytes=64)
+        gate_cols = keep.tile([P, 2 * turned_tokens // P], F32, name="gate_cols", align_bytes=64)
+        gate_third = keep.tile([P, turned_tokens], F32, name="gate_third", align_bytes=64)
+        direct = [(turned_tokens + a, turned_tokens + b) for a, b in spans(DIRECT)]
+        gate_sb = [keep.tile([P, 3, b - a], F32, name="gate_sb%d" % a, align_bytes=64) for a, b in direct]
         zeros = keep.tile([P, PAD], F32, name="zeros")
         ident = keep.tile([P, P], F32, name="ident", align_bytes=64)
 
@@ -83,6 +87,7 @@ def tile_moe_ecr_mlp_silu_kernel(
         nc.vector.memset(w2s[:].rearrange("p e c -> p (e c)").bitcast(I32), 0)
         nc.vector.memset(x_scales[:].bitcast(I32), 0)
         make_identity(nc, ident[:])
+        nc.gpsimd.memset(gate_rows[:], 0.0)
 
         def load_words(dst, src, e0, e1):
             nc.sync.dma_start(
@@ -114,8 +119,14 @@ def tile_moe_ecr_mlp_silu_kernel(
         load_words(w2, w2_words, 0, E)
         nc.sync.dma_start(pos_sb[1][:], pos2)
         nc.sync.dma_start(pos_sb[2][:], pos3)
-        for n, (a, b) in enumerate(gate_spans):
-            nc.sync.dma_start(gate_sb[n][:], gate.rearrange("r p t -> p r t")[:, :, a:b])
+        by_list = gate.rearrange("r p t -> p r t")
+        nc.sync.dma_start(gate_sb[0][:], by_list[:, :, direct[0][0] : direct[0][1]])
+        nc.sync.dma_start(gate_third[:], gate[2, :, :turned_tokens])
+        for n in range(1, len(direct)):
+            nc.sync.dma_start(gate_sb[n][:], by_list[:, :, direct[n][0] : direct[n][1]])
+        blocks = turned_tokens // P
+        for r in range(2):
+            nc.sync.dma_start(gate_rows[r * blocks : (r + 1) * blocks, :], gate[r, 0, :turned_tokens].rearrange("(b t) -> b t", t=P))
 
         for n, (a, b) in enumerate(x_spans):
             for q0, q1 in spans(X_LOADS[n]):
@@ -202,12 +213,13 @@ def tile_moe_ecr_mlp_silu_kernel(
 
         fetched = [keep.tile([P, T], F32, name="fetched%d" % r, align_bytes=64) for r in range(2)]
         prods = [keep.tile([P, T], F32, name="prod%d" % r, align_bytes=64) for r in range(3)]
-        flipped = keep.tile([P, T], F32, name="flipped", align_bytes=64)
+        weighed = keep.tile([P, blocks, 2, P], F32, name="weighed", align_bytes=64)
+        part = keep.tile([P, T], F32, name="part", align_bytes=64)
         res = keep.tile([P, T], F32, name="res", align_bytes=64)
 
-        def weights(r, a, b):
-            n = max(m for m, span in enumerate(gate_spans) if span[0] <= a)
-            return gate_sb[n][:, r, a - gate_spans[n][0] : b - gate_spans[n][0]]
+        gate_bank = bank(TURN_BANKS[2])
+        nc.tensor.transpose(gate_bank[:, :P], gate_rows[:], ident[:])
+        nc.scalar.copy(gate_cols[:], gate_bank[:, : 2 * blocks])
 
         def named(r, a, b):
             return y[:].indirect(pos_sb[r][:, a // 16 : b // 16])
@@ -215,61 +227,83 @@ def tile_moe_ecr_mlp_silu_kernel(
         def fetch(r, a, b):
             nc.scalar.activation(fetched[r][:, a:b], named(r, a, b), COPY)
 
-        def weigh(r, a, b):
-            nc.vector.tensor_tensor(prods[r][:, a:b], fetched[r][:, a:b], weights(r, a, b), MULT)
+        def add(dst, x0, x1, a, b):
+            nc.vector.tensor_tensor(dst[:, a:b], x0, x1[:, a:b], ADD)
 
-        def fetch_weighed(r, a, b):
-            nc.vector.tensor_tensor(prods[r][:, a:b], named(r, a, b), weights(r, a, b), MULT)
+        def store(a, b):
+            nc.sync.dma_start(out[:, a:b], res[:, a:b])
 
-        def add_turned(acc, r, a, b, first, last):
-            blocks = range(a // P, b // P)
-            for blk in blocks:
-                nc.tensor.matmul(
-                    acc[:, blk * P - a : (blk + 1) * P - a], prods[r][:, blk * P : (blk + 1) * P], ident[:],
-                    start=first and blk == blocks[0], stop=last and blk == blocks[-1], is_transpose=True,
-                )
+        chunks = spans(TURNED)
+        by_token, back = {}, {}
 
-        def turn_back(acc, back, a, b):
-            nc.scalar.copy(flipped[:, a:b], acc)
-            for blk in range(a // P, b // P):
-                nc.tensor.transpose(back[:, blk * P - a : (blk + 1) * P - a], flipped[:, blk * P : (blk + 1) * P], ident[:])
+        def fetch_and_turn(n):
+            a, b = chunks[n]
+            by_token[n] = bank(n)[:, : 2 * (b - a)].rearrange("t (r c) -> t r c", r=2)
+            for r in range(2):
+                fetch(r, a, b)
+                for c in range(0, b - a, P):
+                    nc.tensor.transpose(by_token[n][:, r, c : c + P], fetched[r][:, a + c : a + c + P], ident[:])
 
-        def leave(back, a, b):
-            nc.scalar.copy(res[:, a:b], back)
-            nc.scalar.dma_start(out[:, a:b], res[:, a:b])
+        def weigh_and_turn_back(n):
+            a, b = chunks[n]
+            back[n] = bank(len(chunks) + n)[:, : b - a]
+            for c in range(0, b - a, P):
+                blk = (a + c) // P
+                for r in range(2):
+                    nc.scalar.activation(
+                        weighed[:, blk, r, :], by_token[n][:, r, c : c + P], COPY, scale=gate_cols[:, r * blocks + blk : r * blocks + blk + 1]
+                    )
+                    nc.tensor.matmul(back[n][:, c : c + P], weighed[:, blk, r, :], ident[:], start=(r == 0), stop=(r == 1), is_transpose=True)
 
-        chunks = spans(SUMMED)
-        start = sum(SUMMED)
-        last = T - ADDED[-1]
-        sums = [bank(n)[:, : b - a] for n, (a, b) in enumerate(chunks)]
-        backs = [bank(len(chunks) + n)[:, : b - a] for n, (a, b) in enumerate(chunks)]
-        for a, b in chunks:
-            fetch(0, a, b)
-        for n, (a, b) in enumerate(chunks):
-            fetch_weighed(1, a, b)
-            add_turned(sums[n], 1, a, b, True, False)
-            fetch_weighed(2, a, b)
-            add_turned(sums[n], 2, a, b, False, False)
-            weigh(0, a, b)
-            add_turned(sums[n], 0, a, b, False, True)
-        turn_back(sums[0], backs[0], *chunks[0])
-        fetch(0, start, T)
-        leave(backs[0], *chunks[0])
-        turn_back(sums[1], backs[1], *chunks[1])
-        fetch(1, start, T)
-        leave(backs[1], *chunks[1])
-        turn_back(sums[2], backs[2], *chunks[2])
-        leave(backs[2], *chunks[2])
+        def finish_turned(n):
+            add(res, back[n], prods[2], *chunks[n])
+            store(*chunks[n])
 
-        part = keep.tile([P, T - start], F32, name="part", align_bytes=64)
-        fetch_weighed(2, start, last)
-        weigh(0, start, T)
-        weigh(1, start, last)
-        nc.vector.tensor_tensor(part[:, : last - start], prods[2][:, start:last], prods[0][:, start:last], ADD)
-        weigh(1, last, T)
-        nc.vector.tensor_tensor(res[:, start:last], part[:, : last - start], prods[1][:, start:last], ADD)
-        nc.sync.dma_start(out[:, start:last], res[:, start:last])
-        nc.vector.tensor_tensor(part[:, last - start :], prods[0][:, last:T], prods[1][:, last:T], ADD)
-        fetch_weighed(2, last, T)
-        nc.vector.tensor_tensor(res[:, last:T], part[:, last - start :], prods[2][:, last:T], ADD)
-        nc.sync.dma_start(out[:, last:T], res[:, last:T])
+        def product(r, n):
+            a, b = direct[n]
+            nc.vector.tensor_tensor(prods[r][:, a:b], named(r, a, b), gate_sb[n][:, r, :], MULT)
+
+        def weigh(r, n):
+            a, b = direct[n]
+            nc.vector.tensor_tensor(prods[r][:, a:b], fetched[r][:, a:b], gate_sb[n][:, r, :], MULT)
+
+        def third(a, b):
+            nc.vector.tensor_tensor(prods[2][:, a:b], named(2, a, b), gate_third[:, a:b], MULT)
+
+        def add_two(n):
+            a, b = direct[n]
+            add(part, prods[0][:, a:b], prods[1], a, b)
+
+        def finish_direct(n):
+            a, b = direct[n]
+            add(res, part[:, a:b], prods[2], a, b)
+            store(a, b)
+
+        fetch_and_turn(0)
+        fetch_and_turn(1)
+        weigh_and_turn_back(0)
+        fetch_and_turn(2)
+        weigh_and_turn_back(1)
+        fetch(0, *direct[2])
+        fetch(1, *direct[2])
+        weigh_and_turn_back(2)
+
+        for r in range(3):
+            product(r, 0)
+        add_two(0)
+        third(0, turned_tokens // 2)
+        finish_direct(0)
+        third(turned_tokens // 2, turned_tokens)
+        finish_turned(0)
+        product(0, 1)
+        product(1, 1)
+        finish_turned(1)
+        add_two(1)
+        product(2, 1)
+        weigh(0, 2)
+        finish_direct(1)
+        weigh(1, 2)
+        finish_turned(2)
+        add_two(2)
+        product(2, 2)
+        finish_direct(2)

@@ -24,16 +24,14 @@ MULT = mybir.AluOpType.mult
 ADD = mybir.AluOpType.add
 
 X_LOADS = [[512, 128], [256, 256], [256], [128]]
-SCALE_RUNS = [8, 4]
+SCALE_RUNS = [4, 4, 4]
 SCALE_CUTS = [256, 384, 384, 256, 256]
 WORD_CUTS = [192, 192, 384, 384, 384]
 GROUPS = [2, 2, 2, 2, 2, 1, 1]
 VECTOR_GROUPS = 4
-RING = 4
-TURN_LAG = 2
-TURN_BANKS = [4, 5, 6, 8 % RING, 7, 10 % RING, 11 % RING]
-TURNED = [256, 256, 256]
-DIRECT = [384, 256, 128]
+RING = 8
+TURN_BANKS = [4, 5, 8 % RING, 9 % RING, 6, 7, 11 % RING]
+PIECES = [("direct", 384), ("direct", 256), ("turned", 256), ("turned", 256), ("turned", 256), ("direct", 128)]
 
 
 def spans(widths):
@@ -71,12 +69,14 @@ def tile_moe_ecr_mlp_silu_kernel(
         h_rows = [keep.tile([P, H], BF16, name="h_rows%d" % e, align_bytes=64) for e in range(E)]
         h_scales = keep.tile([P, S], U8, name="h_scales", align_bytes=64)
         y = keep.tile([P, S + PAD], F32, name="y", align_bytes=64)
-        turned_tokens = sum(TURNED)
+        pieces = spans([width for kind, width in PIECES])
+        chunks = [span for span, (kind, width) in zip(pieces, PIECES) if kind == "turned"]
+        direct = [span for span, (kind, width) in zip(pieces, PIECES) if kind == "direct"]
         gate_rows = keep.tile([P, P], F32, name="gate_rows", align_bytes=64)
-        gate_cols = keep.tile([P, 2 * turned_tokens // P], F32, name="gate_cols", align_bytes=64)
-        gate_third = keep.tile([P, turned_tokens], F32, name="gate_third", align_bytes=64)
-        direct = [(turned_tokens + a, turned_tokens + b) for a, b in spans(DIRECT)]
-        gate_sb = [keep.tile([P, 3, b - a], F32, name="gate_sb%d" % a, align_bytes=64) for a, b in direct]
+        gate_cols = keep.tile([P, 4 * len(chunks)], F32, name="gate_cols", align_bytes=64)
+        gate_third = keep.tile([P, T], F32, name="gate_third", align_bytes=64)
+        gate_first = keep.tile([P, 2, chunks[0][0]], F32, name="gate_first", align_bytes=64)
+        gate_last = keep.tile([P, 2, T - direct[2][0]], F32, name="gate_last", align_bytes=64)
         zeros = keep.tile([P, PAD], F32, name="zeros")
         ident = keep.tile([P, P], F32, name="ident", align_bytes=64)
 
@@ -110,23 +110,23 @@ def tile_moe_ecr_mlp_silu_kernel(
         load_words(w1, w1_words, 0, 1)
         load_words(w1, w1_words, 1, 2)
         nc.sync.dma_start(pos_sb[0][:], pos1)
-        (first_run, second_run), half = spans(SCALE_RUNS), E // 2
-        load_scales(w1s_runs[0], w1_scales, *first_run)
-        load_words(w1, w1_words, 2, half)
-        load_words(w1, w1_words, half, E)
-        load_scales(w1s_runs[1], w1_scales, *second_run)
+        runs = spans(SCALE_RUNS)
+        load_scales(w1s_runs[0], w1_scales, *runs[0])
+        load_words(w1, w1_words, 2, runs[0][1])
+        for n in range(1, len(runs)):
+            load_words(w1, w1_words, *runs[n])
+            load_scales(w1s_runs[n], w1_scales, *runs[n])
         load_scales(w2s, w2_scales, 0, E)
         load_words(w2, w2_words, 0, E)
+        blocks = 2 * len(chunks)
+        for r in range(2):
+            nc.sync.dma_start(gate_rows[r * blocks : (r + 1) * blocks, :], gate[r, 0, chunks[0][0] : chunks[-1][1]].rearrange("(c t) -> c t", t=P))
+        by_list = gate.rearrange("r p t -> p r t")
+        nc.sync.dma_start(gate_first[:], by_list[:, :2, : chunks[0][0]])
+        nc.sync.dma_start(gate_third[:], gate[2])
         nc.sync.dma_start(pos_sb[1][:], pos2)
         nc.sync.dma_start(pos_sb[2][:], pos3)
-        by_list = gate.rearrange("r p t -> p r t")
-        nc.sync.dma_start(gate_sb[0][:], by_list[:, :, direct[0][0] : direct[0][1]])
-        nc.sync.dma_start(gate_third[:], gate[2, :, :turned_tokens])
-        for n in range(1, len(direct)):
-            nc.sync.dma_start(gate_sb[n][:], by_list[:, :, direct[n][0] : direct[n][1]])
-        blocks = turned_tokens // P
-        for r in range(2):
-            nc.sync.dma_start(gate_rows[r * blocks : (r + 1) * blocks, :], gate[r, 0, :turned_tokens].rearrange("(b t) -> b t", t=P))
+        nc.sync.dma_start(gate_last[:], by_list[:, :2, direct[2][0] :])
 
         for n, (a, b) in enumerate(x_spans):
             for q0, q1 in spans(X_LOADS[n]):
@@ -192,118 +192,112 @@ def tile_moe_ecr_mlp_silu_kernel(
         for word_span, scale_span in zip(word_spans[1:], scale_spans[1:]):
             gather(slot_codes, x_codes, *word_span)
             gather(slot_scales, x_scales, *scale_span)
-        for pair in range(E // 2):
-            layer1(2 * pair)
-            layer1(2 * pair + 1)
-            if pair >= TURN_LAG:
-                turn(pair - TURN_LAG)
-        for g in range(E // 2 - TURN_LAG, len(groups)):
+        for e in range(RING):
+            layer1(e)
+        turn(0)
+        turn(1)
+        for e in range(RING, E):
+            layer1(e)
+        for g in range(2, len(groups)):
             turn(g)
         for g in range(len(groups)):
             unload(g, nc.vector.tensor_copy if g < VECTOR_GROUPS else nc.scalar.copy)
             if g:
                 quantise(g - 1)
         quantise(len(groups) - 1)
-        layer2(0, 2, 9 % RING, nc.scalar.copy)
-        layer2(2, 6, TURN_BANKS[2], nc.scalar.copy)
-        layer2(6, 8, TURN_BANKS[3], nc.vector.tensor_copy)
-        layer2(8, 10, TURN_BANKS[0], nc.vector.tensor_copy)
-        layer2(10, 11, TURN_BANKS[1], nc.scalar.copy)
+        layer2(0, 4, 10 % RING, nc.scalar.copy)
+        layer2(4, 6, TURN_BANKS[0], nc.scalar.copy)
+        layer2(6, 8, TURN_BANKS[1], nc.vector.tensor_copy)
+        layer2(8, 10, TURN_BANKS[2], nc.vector.tensor_copy)
+        layer2(10, 11, TURN_BANKS[3], nc.scalar.copy)
         layer2(11, 12, TURN_BANKS[4], nc.scalar.copy)
 
-        fetched = [keep.tile([P, T], F32, name="fetched%d" % r, align_bytes=64) for r in range(2)]
         prods = [keep.tile([P, T], F32, name="prod%d" % r, align_bytes=64) for r in range(3)]
-        weighed = keep.tile([P, blocks, 2, P], F32, name="weighed", align_bytes=64)
+        weighed = keep.tile([P, len(chunks), 2, 2, P], F32, name="weighed", align_bytes=64)
         part = keep.tile([P, T], F32, name="part", align_bytes=64)
         res = keep.tile([P, T], F32, name="res", align_bytes=64)
 
-        gate_bank = bank(TURN_BANKS[2])
+        gate_bank = bank(TURN_BANKS[5])
         nc.tensor.transpose(gate_bank[:, :P], gate_rows[:], ident[:])
-        nc.scalar.copy(gate_cols[:], gate_bank[:, : 2 * blocks])
+        nc.scalar.copy(gate_cols[:], gate_bank[:, : 4 * len(chunks)])
 
         def named(r, a, b):
             return y[:].indirect(pos_sb[r][:, a // 16 : b // 16])
 
-        def fetch(r, a, b):
-            nc.scalar.activation(fetched[r][:, a:b], named(r, a, b), COPY)
+        def fetch(r, a, b, name):
+            fetched = keep.tile([P, b - a], F32, name=name, align_bytes=64)
+            nc.scalar.activation(fetched[:], named(r, a, b), COPY)
+            return fetched
 
         def add(dst, x0, x1, a, b):
-            nc.vector.tensor_tensor(dst[:, a:b], x0, x1[:, a:b], ADD)
+            nc.vector.tensor_tensor(dst[:, a:b], x0, x1, ADD)
 
         def store(a, b):
             nc.sync.dma_start(out[:, a:b], res[:, a:b])
 
-        chunks = spans(TURNED)
-        by_token, back = {}, {}
+        by_token = [bank(n)[:].rearrange("t (r c m) -> t r c m", r=2, m=P) for n in range(len(chunks))]
+        back = {}
 
-        def fetch_and_turn(n):
-            a, b = chunks[n]
-            by_token[n] = bank(n)[:, : 2 * (b - a)].rearrange("t (r c) -> t r c", r=2)
-            for r in range(2):
-                fetch(r, a, b)
-                for c in range(0, b - a, P):
-                    nc.tensor.transpose(by_token[n][:, r, c : c + P], fetched[r][:, a + c : a + c + P], ident[:])
+        def turn_fetched(r, n, fetched):
+            for c in range(2):
+                nc.tensor.transpose(by_token[n][:, r, c, :], fetched[:, c * P : (c + 1) * P], ident[:])
+
+        def fetch_second(n):
+            turn_fetched(1, n, fetch(1, *chunks[n], "second%d" % n))
 
         def weigh_and_turn_back(n):
-            a, b = chunks[n]
-            back[n] = bank(len(chunks) + n)[:, : b - a]
-            for c in range(0, b - a, P):
-                blk = (a + c) // P
+            back[n] = bank(len(chunks) + n)[:, : 2 * P]
+            for c in range(2):
                 for r in range(2):
-                    nc.scalar.activation(
-                        weighed[:, blk, r, :], by_token[n][:, r, c : c + P], COPY, scale=gate_cols[:, r * blocks + blk : r * blocks + blk + 1]
-                    )
-                    nc.tensor.matmul(back[n][:, c : c + P], weighed[:, blk, r, :], ident[:], start=(r == 0), stop=(r == 1), is_transpose=True)
+                    col = r * blocks + 2 * n + c
+                    nc.scalar.activation(weighed[:, n, c, r, :], by_token[n][:, r, c, :], COPY, scale=gate_cols[:, col : col + 1])
+                    nc.tensor.matmul(back[n][:, c * P : (c + 1) * P], weighed[:, n, c, r, :], ident[:], start=(r == 0), stop=(r == 1), is_transpose=True)
 
-        def finish_turned(n):
-            add(res, back[n], prods[2], *chunks[n])
-            store(*chunks[n])
+        def product(r, a, b):
+            nc.vector.tensor_tensor(prods[r][:, a:b], named(r, a, b), gate_first[:, r, a:b], MULT)
 
-        def product(r, n):
-            a, b = direct[n]
-            nc.vector.tensor_tensor(prods[r][:, a:b], named(r, a, b), gate_sb[n][:, r, :], MULT)
+        def weigh(r, fetched):
+            nc.vector.tensor_tensor(prods[r][:, last:], fetched, gate_last[:, r, :], MULT)
 
-        def weigh(r, n):
-            a, b = direct[n]
-            nc.vector.tensor_tensor(prods[r][:, a:b], fetched[r][:, a:b], gate_sb[n][:, r, :], MULT)
+        def third(a, b, dst):
+            nc.vector.tensor_tensor(dst, named(2, a, b), gate_third[:, a:b], MULT)
 
-        def third(a, b):
-            nc.vector.tensor_tensor(prods[2][:, a:b], named(2, a, b), gate_third[:, a:b], MULT)
+        def add_two(a, b):
+            add(part, prods[0][:, a:b], prods[1][:, a:b], a, b)
 
-        def add_two(n):
-            a, b = direct[n]
-            add(part, prods[0][:, a:b], prods[1], a, b)
-
-        def finish_direct(n):
-            a, b = direct[n]
-            add(res, part[:, a:b], prods[2], a, b)
-            store(a, b)
-
-        fetch_and_turn(0)
-        fetch_and_turn(1)
+        c0, c1, c2 = (a for a, b in chunks)
+        cut, last = direct[1][0], direct[2][0]
+        first = fetch(0, c0, T, "first")
+        for n, (a, b) in enumerate(chunks):
+            turn_fetched(0, n, first[:, a - c0 : b - c0])
+        fetch_second(0)
+        fetch_second(1)
         weigh_and_turn_back(0)
-        fetch_and_turn(2)
+        fetch_second(2)
         weigh_and_turn_back(1)
-        fetch(0, *direct[2])
-        fetch(1, *direct[2])
         weigh_and_turn_back(2)
+        late = fetch(1, last, T, "second2")
 
-        for r in range(3):
-            product(r, 0)
-        add_two(0)
-        third(0, turned_tokens // 2)
-        finish_direct(0)
-        third(turned_tokens // 2, turned_tokens)
-        finish_turned(0)
-        product(0, 1)
-        product(1, 1)
-        finish_turned(1)
-        add_two(1)
-        product(2, 1)
-        weigh(0, 2)
-        finish_direct(1)
-        weigh(1, 2)
-        finish_turned(2)
-        add_two(2)
-        product(2, 2)
-        finish_direct(2)
+        product(0, 0, c0)
+        product(1, 0, cut)
+        third(0, c0, prods[2][:, :c0])
+        add_two(0, cut)
+        product(1, cut, c0)
+        add(res, part[:, :cut], prods[2][:, :cut], 0, cut)
+        store(0, cut)
+        third(c0, c2, prods[2][:, c0:c2])
+        add_two(cut, c0)
+        add(res, back[0], prods[2][:, c0:c1], c0, c1)
+        add(res, part[:, cut:c0], prods[2][:, cut:c0], cut, c0)
+        store(cut, c1)
+        third(c2, last, prods[2][:, c2:last])
+        add(res, back[1], prods[2][:, c1:c2], c1, c2)
+        weigh(0, first[:, last - c0 :])
+        add(res, back[2], prods[2][:, c2:last], c2, last)
+        store(c1, last)
+        reused = prods[2][:, c2 : c2 + T - last]
+        weigh(1, late[:])
+        third(last, T, reused)
+        add_two(last, T)
+        add(res, part[:, last:], reused, last, T)
+        store(last, T)

@@ -23,7 +23,7 @@ COPY = mybir.ActivationFunctionType.Copy
 MULT = mybir.AluOpType.mult
 ADD = mybir.AluOpType.add
 
-X_LOADS = [[512, 128], [256, 256], [256], [128]]
+X_LOADS = [[512], [128], [256, 256], [256], [128]]
 SCALE_RUNS = [4, 4, 4]
 SCALE_CUTS = [256, 384, 384, 256, 256]
 WORD_CUTS = [192, 192, 384, 384, 384]
@@ -109,7 +109,6 @@ def tile_moe_ecr_mlp_silu_kernel(
         nc.sync.dma_start(offs_sb[:], offs)
         load_words(w1, w1_words, 0, 1)
         load_words(w1, w1_words, 1, 2)
-        nc.sync.dma_start(pos_sb[0][:], pos1)
         runs = spans(SCALE_RUNS)
         load_scales(w1s_runs[0], w1_scales, *runs[0])
         load_words(w1, w1_words, 2, runs[0][1])
@@ -124,8 +123,8 @@ def tile_moe_ecr_mlp_silu_kernel(
         by_list = gate.rearrange("r p t -> p r t")
         nc.sync.dma_start(gate_first[:], by_list[:, :2, : chunks[0][0]])
         nc.sync.dma_start(gate_third[:], gate[2])
-        nc.sync.dma_start(pos_sb[1][:], pos2)
-        nc.sync.dma_start(pos_sb[2][:], pos3)
+        for r, pos in enumerate((pos1, pos2, pos3)):
+            nc.sync.dma_start(pos_sb[r][:], pos)
         nc.sync.dma_start(gate_last[:], by_list[:, :2, direct[2][0] :])
 
         for n, (a, b) in enumerate(x_spans):
@@ -224,10 +223,8 @@ def tile_moe_ecr_mlp_silu_kernel(
         def named(r, a, b):
             return y[:].indirect(pos_sb[r][:, a // 16 : b // 16])
 
-        def fetch(r, a, b, name):
-            fetched = keep.tile([P, b - a], F32, name=name, align_bytes=64)
-            nc.scalar.activation(fetched[:], named(r, a, b), COPY)
-            return fetched
+        def fetch(dst, r, a, b):
+            nc.scalar.activation(dst, named(r, a, b), COPY)
 
         def add(dst, x0, x1, a, b):
             nc.vector.tensor_tensor(dst[:, a:b], x0, x1, ADD)
@@ -242,8 +239,11 @@ def tile_moe_ecr_mlp_silu_kernel(
             for c in range(2):
                 nc.tensor.transpose(by_token[n][:, r, c, :], fetched[:, c * P : (c + 1) * P], ident[:])
 
-        def fetch_second(n):
-            turn_fetched(1, n, fetch(1, *chunks[n], "second%d" % n))
+        def fetch_and_turn(n):
+            for r in range(2):
+                fetched = keep.tile([P, 2 * P], F32, name="fetched%d_%d" % (r, n), align_bytes=64)
+                fetch(fetched[:], r, *chunks[n])
+                turn_fetched(r, n, fetched)
 
         def weigh_and_turn_back(n):
             back[n] = bank(len(chunks) + n)[:, : 2 * P]
@@ -267,16 +267,15 @@ def tile_moe_ecr_mlp_silu_kernel(
 
         c0, c1, c2 = (a for a, b in chunks)
         cut, last = direct[1][0], direct[2][0]
-        first = fetch(0, c0, T, "first")
-        for n, (a, b) in enumerate(chunks):
-            turn_fetched(0, n, first[:, a - c0 : b - c0])
-        fetch_second(0)
-        fetch_second(1)
+        fetch_and_turn(0)
+        fetch_and_turn(1)
         weigh_and_turn_back(0)
-        fetch_second(2)
+        fetch_and_turn(2)
         weigh_and_turn_back(1)
         weigh_and_turn_back(2)
-        late = fetch(1, last, T, "second2")
+        late = [weighed[:, 1, 1, r, :] for r in range(2)]
+        for r in range(2):
+            fetch(late[r], r, last, T)
 
         product(0, 0, c0)
         product(1, 0, cut)
@@ -292,11 +291,11 @@ def tile_moe_ecr_mlp_silu_kernel(
         store(cut, c1)
         third(c2, last, prods[2][:, c2:last])
         add(res, back[1], prods[2][:, c1:c2], c1, c2)
-        weigh(0, first[:, last - c0 :])
+        weigh(0, late[0])
         add(res, back[2], prods[2][:, c2:last], c2, last)
         store(c1, last)
         reused = prods[2][:, c2 : c2 + T - last]
-        weigh(1, late[:])
+        weigh(1, late[1])
         third(last, T, reused)
         add_two(last, T)
         add(res, part[:, last:], reused, last, T)

@@ -74,9 +74,9 @@ def tile_moe_ecr_mlp_silu_kernel(
         direct = [span for span, (kind, width) in zip(pieces, PIECES) if kind == "direct"]
         gate_rows = keep.tile([P, P], F32, name="gate_rows", align_bytes=64)
         gate_cols = keep.tile([P, 4 * len(chunks)], F32, name="gate_cols", align_bytes=64)
-        gate_third = keep.tile([P, T], F32, name="gate_third", align_bytes=64)
+        gate_third = keep.tile([P, direct[2][0]], F32, name="gate_third", align_bytes=64)
         gate_first = keep.tile([P, 2, chunks[0][0]], F32, name="gate_first", align_bytes=64)
-        gate_last = keep.tile([P, 2, T - direct[2][0]], F32, name="gate_last", align_bytes=64)
+        gate_last = keep.tile([P, 3, T - direct[2][0]], F32, name="gate_last", align_bytes=64)
         zeros = keep.tile([P, PAD], F32, name="zeros")
         ident = keep.tile([P, P], F32, name="ident", align_bytes=64)
 
@@ -122,10 +122,10 @@ def tile_moe_ecr_mlp_silu_kernel(
             nc.sync.dma_start(gate_rows[r * blocks : (r + 1) * blocks, :], gate[r, 0, chunks[0][0] : chunks[-1][1]].rearrange("(c t) -> c t", t=P))
         by_list = gate.rearrange("r p t -> p r t")
         nc.sync.dma_start(gate_first[:], by_list[:, :2, : chunks[0][0]])
-        nc.sync.dma_start(gate_third[:], gate[2])
+        nc.sync.dma_start(gate_third[:], gate[2, :, : direct[2][0]])
         for r, pos in enumerate((pos1, pos2, pos3)):
             nc.sync.dma_start(pos_sb[r][:], pos)
-        nc.sync.dma_start(gate_last[:], by_list[:, :2, direct[2][0] :])
+        nc.sync.dma_start(gate_last[:], by_list[:, :, direct[2][0] :])
 
         for n, (a, b) in enumerate(x_spans):
             for q0, q1 in spans(X_LOADS[n]):
@@ -267,14 +267,12 @@ def tile_moe_ecr_mlp_silu_kernel(
 
         c0, c1, c2 = (a for a, b in chunks)
         cut, last = direct[1][0], direct[2][0]
-        fetch_and_turn(0)
-        fetch_and_turn(1)
-        weigh_and_turn_back(0)
-        fetch_and_turn(2)
-        weigh_and_turn_back(1)
-        weigh_and_turn_back(2)
-        late = [weighed[:, 1, 1, r, :] for r in range(2)]
-        for r in range(2):
+        for n in range(len(chunks)):
+            fetch_and_turn(n)
+        for n in range(len(chunks)):
+            weigh_and_turn_back(n)
+        late = [weighed[:, 1, 1, 0, :], weighed[:, 1, 1, 1, :], weighed[:, 1, 0, 1, :]]
+        for r in range(3):
             fetch(late[r], r, last, T)
 
         product(0, 0, c0)
@@ -294,9 +292,8 @@ def tile_moe_ecr_mlp_silu_kernel(
         weigh(0, late[0])
         add(res, back[2], prods[2][:, c2:last], c2, last)
         store(c1, last)
-        reused = prods[2][:, c2 : c2 + T - last]
         weigh(1, late[1])
-        third(last, T, reused)
+        weigh(2, late[2])
         add_two(last, T)
-        add(res, part[:, last:], reused, last, T)
+        add(res, part[:, last:], prods[2][:, last:], last, T)
         store(last, T)

@@ -25,8 +25,8 @@ ADD = mybir.AluOpType.add
 
 X_LOADS = [[512], [128], [256, 256], [256], [128]]
 SCALE_RUNS = [4, 4, 4]
-SCALE_CUTS = [256, 384, 384, 256, 256]
-WORD_CUTS = [192, 192, 384, 384, 384]
+SCALE_CUTS = [256] * 6
+WORD_CUTS = [128] + [256] * 5 + [128]
 GROUPS = [2, 2, 2, 2, 2, 1, 1]
 VECTOR_GROUPS = 4
 RING = 8
@@ -188,9 +188,10 @@ def tile_moe_ecr_mlp_silu_kernel(
         scale_spans, word_spans = spans(SCALE_CUTS), spans(WORD_CUTS)
         gather(slot_scales, x_scales, *scale_spans[0])
         gather(slot_codes, x_codes, *word_spans[0])
-        for word_span, scale_span in zip(word_spans[1:], scale_spans[1:]):
-            gather(slot_codes, x_codes, *word_span)
-            gather(slot_scales, x_scales, *scale_span)
+        for n in range(1, len(word_spans)):
+            gather(slot_codes, x_codes, *word_spans[n])
+            if n < len(scale_spans):
+                gather(slot_scales, x_scales, *scale_spans[n])
         for e in range(RING):
             layer1(e)
         turn(0)
@@ -206,7 +207,7 @@ def tile_moe_ecr_mlp_silu_kernel(
         quantise(len(groups) - 1)
         layer2(0, 4, 10 % RING, nc.scalar.copy)
         layer2(4, 6, TURN_BANKS[0], nc.scalar.copy)
-        layer2(6, 8, TURN_BANKS[1], nc.vector.tensor_copy)
+        layer2(6, 8, TURN_BANKS[1], nc.scalar.copy)
         layer2(8, 10, TURN_BANKS[2], nc.vector.tensor_copy)
         layer2(10, 11, TURN_BANKS[3], nc.scalar.copy)
         layer2(11, 12, TURN_BANKS[4], nc.scalar.copy)
@@ -271,7 +272,7 @@ def tile_moe_ecr_mlp_silu_kernel(
             fetch_and_turn(n)
         for n in range(len(chunks)):
             weigh_and_turn_back(n)
-        late = [weighed[:, 1, 1, 0, :], weighed[:, 1, 1, 1, :], weighed[:, 1, 0, 1, :]]
+        late = [weighed[:, 0, 0, 0, :], weighed[:, 0, 0, 1, :], weighed[:, 0, 1, 0, :]]
         for r in range(3):
             fetch(late[r], r, last, T)
 

@@ -122,9 +122,9 @@ def tile_moe_ecr_mlp_silu_kernel(
             nc.sync.dma_start(gate_rows[r * blocks : (r + 1) * blocks, :], gate[r, 0, chunks[0][0] : chunks[-1][1]].rearrange("(c t) -> c t", t=P))
         by_list = gate.rearrange("r p t -> p r t")
         nc.sync.dma_start(gate_first[:], by_list[:, :2, : chunks[0][0]])
-        nc.sync.dma_start(gate_third[:], gate[2, :, : direct[2][0]])
         for r, pos in enumerate((pos1, pos2, pos3)):
             nc.sync.dma_start(pos_sb[r][:], pos)
+        nc.sync.dma_start(gate_third[:], gate[2, :, : direct[2][0]])
         nc.sync.dma_start(gate_last[:], by_list[:, :, direct[2][0] :])
 
         for n, (a, b) in enumerate(x_spans):
@@ -278,21 +278,20 @@ def tile_moe_ecr_mlp_silu_kernel(
 
         product(0, 0, c0)
         product(1, 0, cut)
-        third(0, c0, prods[2][:, :c0])
-        add_two(0, cut)
         product(1, cut, c0)
-        add(res, part[:, :cut], prods[2][:, :cut], 0, cut)
-        store(0, cut)
-        third(c0, c2, prods[2][:, c0:c2])
+        add_two(0, cut)
         add_two(cut, c0)
+        third(0, c0, prods[2][:, :c0])
+        third(c0, c2, prods[2][:, c0:c2])
+        add(res, part[:, :c0], prods[2][:, :c0], 0, c0)
+        store(0, c0)
         add(res, back[0], prods[2][:, c0:c1], c0, c1)
-        add(res, part[:, cut:c0], prods[2][:, cut:c0], cut, c0)
-        store(cut, c1)
         third(c2, last, prods[2][:, c2:last])
         add(res, back[1], prods[2][:, c1:c2], c1, c2)
+        store(c0, c2)
         weigh(0, late[0])
         add(res, back[2], prods[2][:, c2:last], c2, last)
-        store(c1, last)
+        store(c2, last)
         weigh(1, late[1])
         weigh(2, late[2])
         add_two(last, T)

@@ -272,7 +272,7 @@ def tile_moe_ecr_mlp_silu_kernel(
             fetch_and_turn(n)
         for n in range(len(chunks)):
             weigh_and_turn_back(n)
-        late = [weighed[:, 0, 0, 0, :], weighed[:, 0, 0, 1, :], weighed[:, 0, 1, 0, :]]
+        late = [weighed[:, 0, 0, 0, :], weighed[:, 0, 0, 1, :], res[:, c2 : c2 + P]]
         for r in range(3):
             fetch(late[r], r, last, T)
 
@@ -289,11 +289,10 @@ def tile_moe_ecr_mlp_silu_kernel(
         third(c2, last, prods[2][:, c2:last])
         add(res, back[1], prods[2][:, c1:c2], c1, c2)
         store(c0, c2)
-        weigh(0, late[0])
+        for r in range(3):
+            weigh(r, late[r])
+        add_two(last, T)
         add(res, back[2], prods[2][:, c2:last], c2, last)
         store(c2, last)
-        weigh(1, late[1])
-        weigh(2, late[2])
-        add_two(last, T)
         add(res, part[:, last:], prods[2][:, last:], last, T)
         store(last, T)

from contextlib import ExitStack

import concourse.mybir as mybir
from concourse.masks import make_identity

K, T, E, C, H, N = 512, 1536, 12, 128, 512, 128
PAD = 64
S = E * C
P = 128
BANK = 512
FLOPS = 2 * S * (K * H + H * N)

F32 = mybir.dt.float32
BF16 = mybir.dt.bfloat16
I32 = mybir.dt.int32
U32 = mybir.dt.uint32
U16 = mybir.dt.uint16
U8 = mybir.dt.uint8
FP8X4 = mybir.dt.float8_e4m3fn_x4
FP4X4 = mybir.dt.float4_e2m1fn_x4
SILU = mybir.ActivationFunctionType.Silu
COPY = mybir.ActivationFunctionType.Copy
MULT = mybir.AluOpType.mult
ADD = mybir.AluOpType.add

X_LOADS = [[512], [128], [256, 256], [256], [128]]
SCALE_RUNS = [4, 4, 4]
SCALE_CUTS = [256] * 6
WORD_CUTS = [128] + [256] * 5 + [128]
GROUPS = [2, 2, 2, 2, 2, 1, 1]
VECTOR_GROUPS = 4
RING = 8
TURN_BANKS = [4, 5, 8 % RING, 9 % RING, 6, 7, 11 % RING]
PIECES = [("direct", 384), ("direct", 256), ("turned", 256), ("turned", 256), ("turned", 256), ("direct", 128)]


def spans(widths):
    pairs, start = [], 0
    for width in widths:
        pairs.append((start, start + width))
        start += width
    return pairs


def tile_moe_ecr_mlp_silu_kernel(
    tc, xT, w1_words, w1_scales, w2_words, w2_scales, gate, offs, pos1, pos2, pos3, out
):
    nc = tc.nc
    with ExitStack() as ctx:
        lists = ctx.enter_context(tc.tile_pool(name="lists", bufs=1))
        keep = ctx.enter_context(tc.tile_pool(name="keep", bufs=1))
        psum = ctx.enter_context(tc.psum_pool(name="psum", bufs=1))

        def bank(b):
            return psum.tile([P, BANK], F32, name="bank%d" % b)

        offs_sb = lists.tile([P, S // 16], U16, name="offs_sb")
        pos_sb = [lists.tile([P, T // 16], U16, name="pos_sb%d" % r) for r in range(3)]

        x_codes = keep.tile([P, T], U32, name="x_codes", align_bytes=64)
        x_scales = keep.tile([P, T], U8, name="x_scales", align_bytes=64)
        slot_codes = keep.tile([P, S], U32, name="slot_codes", align_bytes=64)
        slot_scales = keep.tile([P, S], U8, name="slot_scales", align_bytes=64)
        w1 = keep.tile([P, E, 2 * H], U8, name="w1", align_bytes=64)
        w1s_runs = [keep.tile([P, e1 - e0, H], U8, name="w1s%d" % e0, align_bytes=64) for e0, e1 in spans(SCALE_RUNS)]
        w1s = [run[:, e, :] for run, count in zip(w1s_runs, SCALE_RUNS) for e in range(count)]
        w2 = keep.tile([P, E, 2 * N], U8, name="w2", align_bytes=64)
        w2s = keep.tile([P, E, N], U8, name="w2s", align_bytes=64)
        h_rows = [keep.tile([P, H], BF16, name="h_rows%d" % e, align_bytes=64) for e in range(E)]
        h_scales = keep.tile([P, S], U8, name="h_scales", align_bytes=64)
        y = keep.tile([P, S + PAD], F32, name="y", align_bytes=64)
        pieces = spans([width for kind, width in PIECES])
        chunks = [span for span, (kind, width) in zip(pieces, PIECES) if kind == "turned"]
        direct = [span for span, (kind, width) in zip(pieces, PIECES) if kind == "direct"]
        gate_rows = keep.tile([P, P], F32, name="gate_rows", align_bytes=64)
        gate_cols = keep.tile([P, 4 * len(chunks)], F32, name="gate_cols", align_bytes=64)
        gate_third = keep.tile([P, direct[2][0]], F32, name="gate_third", align_bytes=64)
        gate_first = keep.tile([P, 2, chunks[0][0]], F32, name="gate_first", align_bytes=64)
        gate_last = keep.tile([P, 3, T - direct[2][0]], F32, name="gate_last", align_bytes=64)
        zeros = keep.tile([P, PAD], F32, name="zeros")
        ident = keep.tile([P, P], F32, name="ident", align_bytes=64)

        nc.vector.memset(zeros[:], 0.0)
        nc.scalar.activation(y[:, S:], zeros[:], SILU)
        for run in w1s_runs:
            nc.vector.memset(run[:].rearrange("p e c -> p (e c)").bitcast(I32), 0)
        nc.vector.memset(w2s[:].rearrange("p e c -> p (e c)").bitcast(I32), 0)
        nc.vector.memset(x_scales[:].bitcast(I32), 0)
        make_identity(nc, ident[:])
        nc.gpsimd.memset(gate_rows[:], 0.0)

        def load_words(dst, src, e0, e1):
            nc.sync.dma_start(
                dst[:, e0:e1, :].bitcast(I32),
                src.bitcast(I32).rearrange("e s p c -> p (e s) c")[:, e0:e1, :],
            )

        def load_scales(dst, src, e0, e1):
            rows = src.bitcast(I32).rearrange("e s (q r) c -> r q (e s) c", r=4)
            for r in range(4):
                nc.sync.dma_start(dst[r:P:32, :, :].bitcast(I32), rows[r][:, e0:e1, :])

        x_rows = xT.rearrange("(p j) t -> p j t", j=4)
        x_spans = spans([sum(pieces) for pieces in X_LOADS])
        x_raw = []
        for n, (a, b) in enumerate(x_spans):
            x_raw.append(keep.tile([P, 4, b - a], F32, name="x_raw%d" % n, align_bytes=64))
            nc.sync.dma_start(x_raw[n][:], x_rows[:, :, a:b])
        nc.sync.dma_start(offs_sb[:], offs)
        load_words(w1, w1_words, 0, 1)
        load_words(w1, w1_words, 1, 2)
        runs = spans(SCALE_RUNS)
        load_scales(w1s_runs[0], w1_scales, *runs[0])
        load_words(w1, w1_words, 2, runs[0][1])
        for n in range(1, len(runs)):
            load_words(w1, w1_words, *runs[n])
            load_scales(w1s_runs[n], w1_scales, *runs[n])
        load_scales(w2s, w2_scales, 0, E)
        load_words(w2, w2_words, 0, E)
        blocks = 2 * len(chunks)
        for r in range(2):
            nc.sync.dma_start(gate_rows[r * blocks : (r + 1) * blocks, :], gate[r, 0, chunks[0][0] : chunks[-1][1]].rearrange("(c t) -> c t", t=P))
        by_list = gate.rearrange("r p t -> p r t")
        nc.sync.dma_start(gate_first[:], by_list[:, :2, : chunks[0][0]])
        for r, pos in enumerate((pos1, pos2, pos3)):
            nc.sync.dma_start(pos_sb[r][:], pos)
        nc.sync.dma_start(gate_third[:], gate[2, :, : direct[2][0]])
        nc.sync.dma_start(gate_last[:], by_list[:, :, direct[2][0] :])

        for n, (a, b) in enumerate(x_spans):
            for q0, q1 in spans(X_LOADS[n]):
                quads = (q1 - q0) // 4
                xb = keep.tile([P, q1 - q0, 4], BF16, name="xb%d" % (a + q0), align_bytes=64)
                dst = xb[:].rearrange("p (c i) j -> p c j i", i=4)
                src = x_raw[n][:, :, q0:q1].rearrange("p j (c i) -> p c j i", i=4)
                nc.vector.tensor_copy(dst[:, : quads // 2], src[:, : quads // 2])
                nc.scalar.copy(dst[:, quads // 2 :], src[:, quads // 2 :])
                nc.vector.quantize_mx(
                    x_codes[:, a + q0 : a + q1].bitcast(FP8X4), x_scales[:, a + q0 : a + q1], xb[:].rearrange("p t j -> p (t j)")
                )

        def gather(dst, src, a, b):
            nc.vector.tensor_copy(dst[:, a:b], src[:].indirect(offs_sb[:, a // 16 : b // 16]))

        def layer1(e):
            cols = slice(e * C, (e + 1) * C)
            acc = bank(e % RING)[:]
            nc.tensor.matmul_mx(
                acc, slot_codes[:, cols].bitcast(FP8X4), slot_scales[:, cols],
                w1[:, e, :].bitcast(FP4X4), w1s[e], start=True, stop=True,
            )
            nc.scalar.activation(h_rows[e][:].rearrange("s (u p d) -> s u p d", u=2, d=2), acc.rearrange("s (p u d) -> s u p d", u=2, d=2), SILU)

        groups = spans(GROUPS)
        turned, h_cols, h_codes = {}, {}, {}

        def turn(g):
            e0, e1 = groups[g]
            turned[g] = bank(TURN_BANKS[g])[:, : (e1 - e0) * 2 * C].rearrange("p (e u s) -> p e u s", u=2, s=C)
            for e in range(e0, e1):
                units = h_rows[e][:].bitcast(F32)
                for u in range(2):
                    nc.tensor.transpose(turned[g][:, e - e0, u, :], units[:, u * P : (u + 1) * P], ident[:])

        def unload(g, copy):
            e0, e1 = groups[g]
            h_cols[g] = keep.tile([P, (e1 - e0) * 4 * C], BF16, name="h_cols%d" % g, align_bytes=64)
            copy(h_cols[g][:].bitcast(F32).rearrange("p (e s u) -> p e s u", s=C, u=2), turned[g].rearrange("p e u s -> p e s u"))

        def quantise(g):
            e0, e1 = groups[g]
            name = "h_rows%d" % (groups[g + 1][1] - 1) if g + 1 < VECTOR_GROUPS else "h_codes%d" % g
            codes = keep.tile([P, (e1 - e0) * C], U32, name=name, align_bytes=64)
            nc.vector.quantize_mx(codes[:].bitcast(FP8X4), h_scales[:, e0 * C : e1 * C], h_cols[g][:])
            for e in range(e0, e1):
                h_codes[e] = codes[:, (e - e0) * C : (e - e0 + 1) * C]

        def layer2(e0, e1, b, copy):
            acc = bank(b)[:, : (e1 - e0) * C]
            for e in range(e0, e1):
                cols = slice(e * C, (e + 1) * C)
                nc.tensor.matmul_mx(
                    acc[:, (e - e0) * C : (e - e0 + 1) * C], w2[:, e, :].bitcast(FP4X4), w2s[:, e, :],
                    h_codes[e].bitcast(FP8X4), h_scales[:, cols], start=True, stop=True,
                )
            copy(y[:, e0 * C : e1 * C], acc)

        scale_spans, word_spans = spans(SCALE_CUTS), spans(WORD_CUTS)
        gather(slot_scales, x_scales, *scale_spans[0])
        gather(slot_codes, x_codes, *word_spans[0])
        for n in range(1, len(word_spans)):
            gather(slot_codes, x_codes, *word_spans[n])
            if n < len(scale_spans):
                gather(slot_scales, x_scales, *scale_spans[n])
        for e in range(RING):
            layer1(e)
        turn(0)
        turn(1)
        for e in range(RING, E):
            layer1(e)
        for g in range(2, len(groups)):
            turn(g)
        for g in range(len(groups)):
            unload(g, nc.vector.tensor_copy if g < VECTOR_GROUPS else nc.scalar.copy)
            if g:
                quantise(g - 1)
        quantise(len(groups) - 1)
        layer2(0, 4, 10 % RING, nc.scalar.copy)
        layer2(4, 6, TURN_BANKS[0], nc.scalar.copy)
        layer2(6, 8, TURN_BANKS[1], nc.scalar.copy)
        layer2(8, 10, TURN_BANKS[2], nc.vector.tensor_copy)
        layer2(10, 11, TURN_BANKS[3], nc.scalar.copy)
        layer2(11, 12, TURN_BANKS[4], nc.scalar.copy)

        prods = [keep.tile([P, T], F32, name="prod%d" % r, align_bytes=64) for r in range(3)]
        weighed = keep.tile([P, len(chunks), 2, 2, P], F32, name="weighed", align_bytes=64)
        part = keep.tile([P, T], F32, name="part", align_bytes=64)
        res = keep.tile([P, T], F32, name="res", align_bytes=64)

        gate_bank = bank(TURN_BANKS[5])
        nc.tensor.transpose(gate_bank[:, :P], gate_rows[:], ident[:])
        nc.scalar.copy(gate_cols[:], gate_bank[:, : 4 * len(chunks)])

        def named(r, a, b):
            return y[:].indirect(pos_sb[r][:, a // 16 : b // 16])

        def fetch(dst, r, a, b):
            nc.scalar.activation(dst, named(r, a, b), COPY)

        def add(dst, x0, x1, a, b):
            nc.vector.tensor_tensor(dst[:, a:b], x0, x1, ADD)

        def store(a, b):
            nc.sync.dma_start(out[:, a:b], res[:, a:b])

        by_token = [bank(n)[:].rearrange("t (r c m) -> t r c m", r=2, m=P) for n in range(len(chunks))]
        back = {}

        def turn_fetched(r, n, fetched):
            for c in range(2):
                nc.tensor.transpose(by_token[n][:, r, c, :], fetched[:, c * P : (c + 1) * P], ident[:])

        def fetch_and_turn(n):
            for r in range(2):
                fetched = keep.tile([P, 2 * P], F32, name="fetched%d_%d" % (r, n), align_bytes=64)
                fetch(fetched[:], r, *chunks[n])
                turn_fetched(r, n, fetched)

        def weigh_and_turn_back(n):
            back[n] = bank(len(chunks) + n)[:, : 2 * P]
            for c in range(2):
                for r in range(2):
                    col = r * blocks + 2 * n + c
                    nc.scalar.activation(weighed[:, n, c, r, :], by_token[n][:, r, c, :], COPY, scale=gate_cols[:, col : col + 1])
                    nc.tensor.matmul(back[n][:, c * P : (c + 1) * P], weighed[:, n, c, r, :], ident[:], start=(r == 0), stop=(r == 1), is_transpose=True)

        def product(r, a, b):
            nc.vector.tensor_tensor(prods[r][:, a:b], named(r, a, b), gate_first[:, r, a:b], MULT)

        def weigh(r, fetched):
            nc.vector.tensor_tensor(prods[r][:, last:], fetched, gate_last[:, r, :], MULT)

        def third(a, b, dst):
            nc.vector.tensor_tensor(dst, named(2, a, b), gate_third[:, a:b], MULT)

        def add_two(a, b):
            add(part, prods[0][:, a:b], prods[1][:, a:b], a, b)

        c0, c1, c2 = (a for a, b in chunks)
        cut, last = direct[1][0], direct[2][0]
        for n in range(len(chunks)):
            fetch_and_turn(n)
        for n in range(len(chunks)):
            weigh_and_turn_back(n)
        late = [weighed[:, 0, 0, 0, :], weighed[:, 0, 0, 1, :], res[:, c2 : c2 + P]]
        for r in range(3):
            fetch(late[r], r, last, T)

        product(0, 0, c0)
        product(1, 0, cut)
        product(1, cut, c0)
        add_two(0, cut)
        add_two(cut, c0)
        third(0, c0, prods[2][:, :c0])
        third(c0, c2, prods[2][:, c0:c2])
        add(res, part[:, :c0], prods[2][:, :c0], 0, c0)
        store(0, c0)
        add(res, back[0], prods[2][:, c0:c1], c0, c1)
        third(c2, last, prods[2][:, c2:last])
        add(res, back[1], prods[2][:, c1:c2], c1, c2)
        store(c0, c2)
        for r in range(3):
            weigh(r, late[r])
        add_two(last, T)
        add(res, back[2], prods[2][:, c2:last], c2, last)
        store(c2, last)
        add(res, part[:, last:], prods[2][:, last:], last, T)
        store(last, T)
